import numpy as np, ml_dtypes
CORES = [40,64,80,88,96,104,120,144]
N = 8
BF = ml_dtypes.bfloat16
L, F, M, Q, S, R, C, P = 2048, 256, 512, 3, 2, 3, 64, 8
A, ND, W = L + F, Q * M, L + F + Q * M
def pull(y, ix):
    return np.take_along_axis(y, ix[:, :, None, :], 3)
def evaluate(y, kd, om):
    for l in range(Q):
        i = l * M
        a = pull(y, kd[:, :, i:i + M]); b = pull(y, kd[:, :, ND + i:ND + i + M])
        y[..., A + i:A + i + M] = np.where(om[:, :, None, i:i + M] == 1, np.maximum(a, b), np.minimum(a + b, 255))
def begin(v, kd, om):
    y = np.zeros((N, 8, 16, W), np.int64); y[..., :A] = v
    evaluate(y, kd, om)
    return y
def values(rng, lo, hi):
    return (rng.random((N, 8, 16, A)) * np.exp2(rng.integers(lo, hi + 1, (N, 8, 1, A)))).astype(np.int64)
def kids(rng, near, other):
    k = np.zeros((N, 8, 2, Q, M), np.int64); sh = (N, 8, 2, M)
    for l in range(Q):
        c = rng.random(sh)
        x = rng.integers(A + max(l - 1, 0) * M, A + max(l, 1) * M, sh); z = rng.integers(0, A + l * M, sh); e = rng.integers(0, A, sh)
        k[:, :, :, l] = np.where((c < near) & (l > 0), x, np.where(c < near + other, z, e))
    return k
def aims(rng, v, k, o, share):
    y = begin(v, k.reshape(N, 8, 2 * ND), o)[..., W - M:]
    e = rng.random((N, 8, 1, M)); close = np.clip(y + rng.integers(-20, 21, y.shape), 0, 255)
    far = (rng.random(y.shape) * np.exp2(rng.integers(4, 9, (N, 8, 1, M)))).astype(np.int64)
    return np.where(e < share, y, np.where(e < share + (1 - share) * 0.5, close, far))
def ops(rng, share):
    return (rng.random((N, 8, ND)) < share).astype(np.int64)
def weights(rng, share):
    return (rng.random((N, 8, 16, 2)) < share).astype(np.int64)
def pack(v, k, o, g, w):
    return {"lv": np.ascontiguousarray(v.reshape(N, 128, A)).astype(np.float32).astype(BF), "kid": np.ascontiguousarray(k.reshape(N, 8, 2 * ND)).astype(np.int32),
            "mx": np.ascontiguousarray(o).astype(np.int32), "tg": np.ascontiguousarray(g.reshape(N, 128, M)).astype(np.float32).astype(BF),
            "wt": np.ascontiguousarray(w.reshape(N, 128, 2)).astype(np.int32)}
def setup_inputs(rng):
    v = values(rng, 4, 8); k = kids(rng, 0.5, 0.25); o = ops(rng, 0.4)
    return pack(v, k, o, aims(rng, v, k, o, rng.choice(np.array([0.2, 0.5, 0.8, 0.97]), (N, 8, 1, 1))), weights(rng, 0.6))
def setup_inputs_room(rng):
    v = rng.integers(1, 128, (N, 8, 16, A)); v[..., L:L + 2] = 0; v[:, :, 0, L + 1] = 1
    k = kids(rng, 0.5, 0.25); o = ops(rng, 0.4); w = weights(rng, 0.6)
    k[:, :, :, Q - 1] = rng.integers(0, A, (N, 8, 2, M)); o[:, :, ND - M:] = 0
    g = pull(v, k[:, :, 0, Q - 1]) + pull(v, k[:, :, 1, Q - 1])
    for q in range(N):
        for j in range(8):
            n = int(rng.choice(np.array([0, 1, C - 1, C, C + 1, M])))
            if q == 0: n = (C, C + 1, M, C - 1, 1, 0, C, C + 1)[j]
            at = np.arange(M - n, M) if q == 0 and j < 4 else rng.permutation(M)[:n]
            k[q, j, :, Q - 1, at] = L; g[q, j, :, at] = rng.integers(128, 256, (n, 16))
    k[0, 0:4:3, 1, Q - 1, M - 1] = L + 1; o[0, 0:4:3, ND - 1] = 1
    return pack(v, k, o, g, w)
def setup_inputs_ties(rng):
    few = np.array([0, 1, 2, 127, 128, 254, 255]); pal = rng.choice(few, (N, 8, 16, 6)).astype(np.int64)
    v = pull(pal, rng.integers(0, 6, (N, 8, A))); k = kids(rng, 0.4, 0.2)
    k[:, :, 1] = np.where(rng.random((N, 8, Q, M)) < 0.3, k[:, :, 0], k[:, :, 1])
    g = np.where(rng.random((N, 8, 1, M)) < 0.5, pull(pal, rng.integers(0, 6, (N, 8, M))), rng.choice(few, (N, 8, 16, M)))
    return pack(v, k, ops(rng, 0.5), g, weights(rng, 0.5))
def setup_inputs_meet(rng):
    v = values(rng, 3, 6); k = kids(rng, 0.5, 0.25)
    for l in range(1, Q):
        some = rng.integers(0, M, (N, 8, 8))
        k[:, :, :, l] = A + (l - 1) * M + np.take_along_axis(some, rng.integers(0, 8, (N, 8, 2 * M)), 2).reshape(N, 8, 2, M)
    k[:, 1::2, :, Q - 1] = k[:, 1::2, :, Q - 1, :1]
    return pack(v, k, ops(rng, 0.7), rng.integers(0, 256, (N, 8, 16, M)), weights(rng, 0.6))
def setup_inputs_ends(rng):
    v = np.where(rng.random((N, 8, 16, A)) < rng.random((N, 8, 1, A)), 255, 0)
    k = kids(rng, 1.0, 0.0); o = ops(rng, 0.5); w = weights(rng, 0.6); w[:, 0::4] = 1; w[:, 1::4] = 0
    for l in range(Q):
        c = [0, L - 1, L, A - 1] + ([A, A + (l - 1) * M, A + l * M - 1] if l else [])
        k[:, 0::2, :, l] = rng.choice(np.array(c), (N, 4, 2, M))
    g = np.where(rng.random((N, 8, 16, M)) < rng.random((N, 8, 1, M)), 255, 0)
    g[..., 0] = 255; g[..., M - 1] = 255; g[..., 1] = 0
    o[..., ND - M] = 1
    for j in (0, 4, 6):
        k[:, j, :, Q - 1, 0] = 0; v[:, j, :, 0] = 0; v[:, j, 0, 1:L] = 255
    w[:, 4] = 1; w[:, 4, 15, 0] = 0; g[:, 4, 15, 0] = 111
    w[:, 6] = 1; w[:, 6, 15, 0] = 0; v[:, 6, :, 1:L] = rng.integers(0, 5, (N, 16, L - 1)); v[:, 6, 0, 1:L] = rng.integers(1, 5, (N, L - 1))
    return pack(v, k, o, g, w)
def setup_inputs_spread(rng):
    v = (rng.random((N, 8, 16, A)) * np.exp2(8 * rng.random((N, 8, 1, A)))).astype(np.int64) * (rng.random((N, 8, 1, A)) > 0.0625)
    near = rng.random((N, 8, 1, 1)); k = kids(rng, near, (1 - near) * rng.random((N, 8, 1, 1))); o = ops(rng, rng.random((N, 8, 1)))
    return pack(v, k, o, aims(rng, v, k, o, rng.random((N, 8, 1, 1))), weights(rng, rng.random((N, 8, 1, 2))))
def check_inputs(d):
    bad = []
    for nm in ("lv", "tg"):
        x = d[nm].astype(np.float32)
        if not (np.min(x) >= 0 and np.max(x) <= 255): bad.append("range of " + nm)
        if np.any(x != np.floor(x)): bad.append("whole numbers in " + nm)
    for nm in ("mx", "wt"):
        if np.min(d[nm]) < 0 or np.max(d[nm]) > 1: bad.append("range of " + nm)
    k = d["kid"].reshape(N, 8, 2, Q, M)
    for l in range(Q):
        if np.min(k[:, :, :, l]) < 0 or np.max(k[:, :, :, l]) >= A + l * M: bad.append("range of kid in level " + str(l))
    return bad
def reference(lv, kid, mx, tg, wt):
    kd = kid.astype(np.int64); om = mx.astype(np.int64)
    y = begin(lv.astype(np.float32).astype(np.int64).reshape(N, 8, 16, A), kd, om)
    goal = tg.astype(np.float32).astype(np.int64).reshape(N, 8, 16, M); w = wt.astype(np.int64).reshape(N, 8, 16, 2)
    for rnd in range(R):
        node = np.tile(ND - M + np.arange(M), (N, 8, 1)); live = np.ones((N, 8, M), bool); want = goal
        par = np.zeros((N, 8, M), np.int64); side = np.zeros((N, 8, M), np.int64); child = np.zeros((N, 8, M), np.int64); err = np.zeros((N, 8, M), np.int64)
        for step in range(S):
            ka = np.take_along_axis(kd, node, 2); kb = np.take_along_axis(kd, node + ND, 2); o = np.take_along_axis(om, node, 2)[:, :, None, :] == 1
            ya = pull(y, ka); yb = pull(y, kb)
            wa = np.where(o, np.where(want >= yb, want, 0), np.maximum(want - yb, 0))
            wb = np.where(o, np.where(want >= ya, want, 0), np.maximum(want - ya, 0))
            ea = np.add.reduce(np.abs(wa - ya), axis=2); eb = np.add.reduce(np.abs(wb - yb), axis=2)
            tob = eb < ea
            par = np.where(live, node, par); side = np.where(live, tob, side); child = np.where(live, np.where(tob, kb, ka), child); err = np.where(live, np.where(tob, eb, ea), err)
            want = np.where(live[:, :, None, :], np.where(tob[:, :, None, :], wb, wa), want)
            live = live & (child >= A); node = np.where(live, child - A, 0)
        u1 = np.add.reduce(w[..., 0:1] * want, axis=2); u2 = np.add.reduce(w[..., 1:2] * want, axis=2)
        h = ((u1 * u2) >> 5) + u2; stride = 2 * (u1 & 127) + 1
        cand = (h[:, :, None, :] + np.arange(P)[None, None, :, None] * stride[:, :, None, :]) & (L - 1)
        off = np.abs(pull(y, cand.reshape(N, 8, P * M)).reshape(N, 8, 16, P, M) - want[:, :, :, None, :])
        ce = np.add.reduce(off, axis=2); m = np.argmin(ce, axis=2)
        donor = np.take_along_axis(cand, m[:, :, None, :], 2)[:, :, 0]
        hit = np.min(ce, axis=2) < err; one = hit.astype(np.int64)
        counts = hit & (np.add.accumulate(one, axis=2) - one < C)
        go = {}
        for q in range(N):
            for g in range(8):
                i = np.flatnonzero(counts[q, g]); go[q, g] = y[q, g][:, child[q, g, i]]
                key, first = np.unique(side[q, g, i] * ND + par[q, g, i], return_index=True)
                kd[q, g, key] = donor[q, g, i[first]]
        for q in range(N):
            for g in range(8):
                v = go[q, g]; y[(q + 1) % N, g, :, rnd * C:rnd * C + v.shape[1]] = v
        evaluate(y, kd, om)
    return {"yo": y.reshape(N, 128, W).astype(np.float32).astype(BF), "ko": kd.astype(np.float32)}

@@ -1,0 +1,593 @@
+from concourse.bass import DstId, RemoteDMATransfer
+from concourse.mybir import dt, AluOpType, AxisListType, ActivationFunctionType
+
+A_ = AluOpType
+F_ = ActivationFunctionType
+
+SCRATCH = {}
+for _n, _w, _t in (
+        ("Y", 3840, "bfloat16"), ("LIBW", 3840, "bfloat16"), ("K", 3136, "bfloat16"), ("KR", 256, "int32"), ("F1", 256, "bfloat16"),
+        ("F2", 256, "bfloat16"), ("MR", 512, "int32"), ("MRB", 512, "bfloat16"), ("SGN", 1536, "bfloat16"), ("D0", 512, "bfloat16"),
+        ("SC0", 512, "bfloat16"), ("T1", 512, "bfloat16"), ("WTI", 2, "int32"), ("CW", 2, "float32"),
+        ("ONE", 512, "bfloat16"), ("IDN", 128, "bfloat16"), ("NI", 128, "bfloat16"), ("HI", 128, "bfloat16"), ("I255", 128, "bfloat16"),
+        ("N256", 128, "bfloat16"), ("N254", 128, "bfloat16"), ("N2", 128, "bfloat16"), ("CMG", 128, "bfloat16"), ("CM1", 128, "bfloat16"),
+        ("G1", 128, "bfloat16"), ("NG", 128, "bfloat16"), ("G1F", 128, "float32"), ("GL", 128, "bfloat16"), ("GP", 128, "bfloat16"),
+        ("CMT", 128, "bfloat16"), ("L8", 2048, "bfloat16"), ("LP", 2048, "bfloat16"), ("X96", 128, "bfloat16"), ("SR1", 1536, "bfloat16"),
+        ("PAR", 128, "bfloat16"), ("XE", 128, "bfloat16"), ("XO", 128, "bfloat16"),
+        ("SR2", 1536, "bfloat16"), ("XQ", 128, "bfloat16"), ("Q3", 384, "bfloat16"), ("KOL", 8, "bfloat16"), ("PI", 8, "int32"), ("PF", 8, "float32"),
+        ("KT", 128, "bfloat16"), ("K1R", 64, "bfloat16"), ("KR0", 64, "float32"), ("DM", 64, "float32"), ("JW", 32, "float32"),
+        ("MT", 256, "bfloat16"), ("KC", 4, "float32"), ("KJ", 4, "float32"),
+        ("GA", 512, "bfloat16"), ("NB", 512, "bfloat16"), ("RB", 512, "bfloat16"), ("VV", 512, "bfloat16"), ("XM", 512, "bfloat16"),
+        ("MD", 512, "bfloat16"), ("TMA", 512, "bfloat16"), ("TMB", 512, "bfloat16"), ("WIN", 1024, "bfloat16"), ("WIN2", 1536, "bfloat16"),
+        ("AB", 1024, "bfloat16"), ("FF", 1024, "bfloat16"), ("SG2", 512, "bfloat16"), ("DN", 512, "bfloat16"), ("DC", 1024, "bfloat16"),
+        ("CG", 1024, "bfloat16"), ("XA0", 1024, "bfloat16"), ("XA1", 1024, "bfloat16"), ("XA2", 1024, "bfloat16"),
+        ("AC0", 1024, "bfloat16"), ("AC1", 1024, "bfloat16"), ("YC", 528, "bfloat16"),
+        ("WR", 2048, "float32"), ("WI", 256, "int32"), ("KWU", 192, "uint16"), ("LU", 64, "uint16"), ("K2U", 64, "uint16"), ("DLU", 32, "uint16"),
+        ("CHU", 32, "uint16"), ("CU", 256, "uint16"), ("CCU", 4, "uint16"), ("JLU", 4, "uint16"), ("OFU", 4, "uint16"),
+        ("BB", 32, "bfloat16"), ("INC", 32, "bfloat16"), ("CMP", 128, "bfloat16"), ("CC16", 4, "bfloat16"), ("PM", 48, "float32"),
+        ("OH", 64, "bfloat16"), ("KEYW", 48, "float32"), ("DONW", 48, "float32"), ("VK", 64, "float32"), ("VD", 64, "float32"),
+        ("SWT", 64, "float32"), ("SGJ", 64, "float32"), ("TQ", 64, "bfloat16"), ("SRC", 64, "bfloat16"), ("MGM", 64, "bfloat16"),
+        ("MGO", 64, "bfloat16"), ("KOB", 3072, "float32")):
+    SCRATCH[_n] = ("sbuf", [128, _w], _t)
+for _k in range(3):
+    for _n in ("SND", "LAND", "RLY"):
+        SCRATCH["%s%d" % (_n, _k)] = ("sbuf", [128, 64], "bfloat16")
+for _k in range(8):
+    SCRATCH["B%d" % _k] = ("psum", [128, 512], "float32")
+
+SEMAPHORES = ["qv", "qa", "qp", "qg"] + ["d%d" % k for k in range(20)] + ["%s%d" % (n, k) for n in ("hop", "arr", "snt", "rst") for k in range(3)]
+
+LIB, LEAF, MN, NODE0 = 2048, 256, 512, 2304
+SOFF = (0, 1024, 512)
+
+
+def ring_relay(topo, core, dst):
+    if topo.may_write(core, dst):
+        return None
+    ok = [h for h in topo.cores_of(core) if h != core and topo.may_write(h, dst)]
+    near = [h for h in ok if topo.die(h) == topo.die(core)]
+    return (near + ok)[0]
+
+
+def bits(topo, src, dst, n):
+    e = topo.engines(src, dst)[:n]
+    return sum(1 << k for k in e), len(e)
+
+
+def relay_program(g, core, T, topo):
+    n = len(T.cores)
+    for r in range(n):
+        dst = T.cores[(r + 1) % n]
+        if ring_relay(topo, T.cores[r], dst) != core:
+            continue
+        _, got = bits(topo, T.cores[r], core, 8)
+        mask, cnt = bits(topo, core, dst, 8)
+        rid, pid = topo.addr(dst, core)
+        for t in range(3):
+            g.wait_ge(T.sem["hop%d" % t], got)
+            g.remote_dma(T["LAND%d" % t][:], T["RLY%d" % t][:], T.sem["arr%d" % t], T.sem["rst%d" % t], pid, rid, mask)
+        for t in range(3):
+            g.wait_ge(T.sem["rst%d" % t], cnt)
+
+
+def rank_program(g, core, T, topo):
+    rank = T.rank_of(core)
+    if rank is None:
+        relay_program(g, core, T, topo)
+        return
+    nr = len(T.cores)
+    dst = T.cores[(rank + 1) % nr]
+    prev = T.cores[(rank - 1) % nr]
+    hop = ring_relay(topo, core, dst)
+    first = dst if hop is None else hop
+    smask, scnt = bits(topo, core, first, 8)
+    srid, spid = topo.addr(first, core)
+    last = ring_relay(topo, prev, core)
+    _, acnt = bits(topo, prev if last is None else last, core, 8)
+
+    eng = {"v": g.vector, "a": g.scalar, "p": g.tensor, "g": g, "s": g.sync}
+    cnt = {"v": 0, "a": 0, "p": 0, "g": 0}
+    clock = {"v": {}, "a": {}, "p": {}, "g": {}, "s": {}}
+    acc = {}
+    nd = [0]
+
+    def waits(q, reads, writes):
+        need = []
+        for lst, wr in ((reads, False), (writes, True)):
+            for nm, a, b in lst:
+                ps = nm[0] == "B" and nm[1:].isdigit()
+                for e in acc.get(nm, ()):
+                    if not ps and (e[1] <= a or e[0] >= b):
+                        continue
+                    if e[2] or wr or (ps and e[3] != q):
+                        if e[3] == q and q != "s" and (wr or (q == "p" and wr)):
+                            if not (e[2] and wr) or q == "p":
+                                continue
+                        if ps and e[3] == q and (e[1] <= a or e[0] >= b):
+                            continue
+                        need.append((e[6], e[4], e[5], e[7]))
+        need.sort(key=lambda x: -x[0])
+        ck = clock[q]
+        for _, sem, val, clk in need:
+            if ck.get(sem, 0) >= val:
+                continue
+            eng[q].wait_ge(T.sem[sem], val)
+            for k in clk:
+                if ck.get(k, 0) < clk[k]:
+                    ck[k] = clk[k]
+            ck[sem] = max(val, ck.get(sem, 0))
+
+    seq = [0]
+
+    def note(q, reads, writes, sem, val):
+        clk = dict(clock[q])
+        clk[sem] = val
+        seq[0] += 1
+        for lst, wr in ((reads, False), (writes, True)):
+            for nm, a, b in lst:
+                old = acc.get(nm, [])
+                if wr:
+                    old = [e for e in old if not (a <= e[0] and e[1] <= b)]
+                else:
+                    old = [e for e in old if not (a <= e[0] and e[1] <= b and not e[2] and e[3] == q)]
+                old.append((a, b, wr, q, sem, val, seq[0], clk))
+                acc[nm] = old
+
+    def op(q, reads, writes, f):
+        waits(q, reads, writes)
+        cnt[q] += 1
+        f().then_inc(T.sem["q" + q], 1)
+        note(q, reads, writes, "q" + q, cnt[q])
+
+    def V(nm, a, b, st=1, p=None):
+        if p is None:
+            ap = T[nm][:, a:b] if st == 1 else T[nm][:, a:b:st]
+        else:
+            ap = T[nm][p[0]:p[1], a:b]
+        return (ap, [(nm, a, b)])
+
+    def IND(win, off):
+        return (win[0].indirect(off[0]), win[1] + off[1])
+
+    def TT(o, x, y, f):
+        op("v", x[1] + y[1], o[1], lambda: g.vector.tensor_tensor(out=o[0], in0=x[0], in1=y[0], op=f))
+
+    def TS(o, x, s1, f1, s2=None, f2=None):
+        rd = list(x[1])
+        a1, a2 = s1, s2
+        if isinstance(s1, tuple):
+            rd += s1[1]
+            a1 = s1[0]
+        if isinstance(s2, tuple):
+            rd += s2[1]
+            a2 = s2[0]
+        if f2 is None:
+            op("v", rd, o[1], lambda: g.vector.tensor_scalar(out=o[0], in0=x[0], scalar1=a1, scalar2=None, op0=f1))
+        else:
+            op("v", rd, o[1], lambda: g.vector.tensor_scalar(out=o[0], in0=x[0], scalar1=a1, scalar2=a2, op0=f1, op1=f2))
+
+    def CP(o, x):
+        op("v", x[1], o[1], lambda: g.vector.tensor_copy(out=o[0], in_=x[0]))
+
+    def RED(o, x):
+        op("v", x[1], o[1], lambda: g.vector.tensor_reduce(out=o[0], in_=x[0], axis=AxisListType.X, op=A_.add))
+
+    def FILL(o, c):
+        op("v", [], o[1], lambda: g.vector.memset(o[0], c))
+
+    def ACT(o, x, f=F_.Copy, bias=None, scale=None, accum=None):
+        rd, wr, kw = list(x[1]), list(o[1]), {}
+        if bias is not None:
+            rd += bias[1]
+            kw["bias"] = bias[0]
+        if scale is not None:
+            if isinstance(scale, tuple):
+                rd += scale[1]
+                kw["scale"] = scale[0]
+            else:
+                kw["scale"] = scale
+        if accum is not None:
+            wr += accum[1]
+            kw["accum_out"] = accum[0]
+        op("a", rd, wr, lambda: g.scalar.activation(out=o[0], in_=x[0], func=f, **kw))
+
+    def MM(o, prs):
+        rd = []
+        for l, r in prs:
+            rd += l[1] + r[1]
+        def f():
+            ins = None
+            for k in range(len(prs)):
+                ins = g.tensor.matmul(o[0], prs[k][0][0], prs[k][1][0], k == 0, k == len(prs) - 1)
+            return ins
+        op("p", rd, o[1], f)
+
+    def IOTA(o, pat, base, ch):
+        op("g", [], o[1], lambda: g.iota(o[0], pat, base, ch, allow_small_or_imprecise_dtypes=True))
+
+    def SEL(o, x, pat, base, ch):
+        op("g", x[1], o[1], lambda: g.affine_select(o[0], x[0], pat, A_.is_equal, 0.0, base, ch))
+
+    def DMA(q, o, x, reads, writes):
+        sem = "d%d" % nd[0]
+        nd[0] += 1
+        waits(q, reads, writes)
+        eng[q].dma_start(out=o, in_=x).then_inc(T.sem[sem], 16)
+        note("dma" + sem, reads, writes, sem, 16)
+
+    for k in range(20):
+        clock["dmad%d" % k] = {}
+
+    def M(nm, p=None):
+        return V(nm, 0, 128, 1, p)
+
+    wtop = [0]
+
+    def w(n=32):
+        a = wtop[0]
+        wtop[0] += n
+        return V("WR", a, a + n)
+
+    def sub(x, a, b):
+        nm, lo, _ = x[1][0]
+        return V(nm, lo + a, lo + b)
+
+    def L(i):
+        return V("L8", 128 * i, 128 * i + 128)
+
+    def diag(out, nm, lo, hi, more=()):
+        MM(out, [(L(i), V(nm, lo + i, hi, 16)) for i in range(16)] + list(more))
+
+    DMA("s", T.KR[0:96, :], T.kid[:], [], [("KR", 0, 256)])
+    DMA("a", T.MR[0:24, :], T.mx[:], [], [("MR", 0, 512)])
+    DMA("s", T.Y[:, 0:NODE0], T.lv[:], [], [("Y", 0, NODE0)])
+    DMA("a", T.D0[:], T.tg[:], [], [("D0", 0, 512)])
+    DMA("a", T.WTI[:], T.wt[:], [], [("WTI", 0, 2)])
+    DMA("s", T.LIBW[:, 0:LIB], T.lv[:, 0:LIB], [], [("LIBW", 0, LIB)])
+    DMA("s", T.LIBW[:, LIB:3840], T.lv[:, 0:1792], [], [("LIBW", LIB, 3840)])
+
+    PI = lambda k: V("PI", k, k + 1)
+    PF = lambda k: V("PF", k, k + 1)
+    FILL(V("ONE", 0, 512), 1.0)
+    op("g", [], PI(0)[1], lambda: g.iota(PI(0)[0], [[0, 1]], 0, 1))
+    IOTA(M("X96"), [[-12, 8], [0, 16]], 0, 1)
+    IOTA(M("PAR"), [[0, 64], [1, 2]], 0, 0)
+    IOTA(M("CMG"), [[1, 8], [0, 16]], 0, 0)
+    IOTA(M("CM1"), [[0, 8], [1, 16]], 1, 0)
+    IOTA(M("XQ"), [[-3, 8], [0, 16]], 0, 1)
+    SEL(M("IDN"), V("ONE", 0, 128), [[-1, 128]], 0, 1)
+    TS(PI(1), PI(0), 4, A_.arith_shift_right)
+    TS(PI(2), PI(0), 15, A_.bitwise_and)
+    TS(PI(3), PI(0), 1, A_.bitwise_and)
+    TS(V("XE", 0, 128), M("PAR"), 200.0, A_.mult)
+    TS(V("XO", 0, 128), M("PAR"), -200.0, A_.mult, 200.0, A_.add)
+    CP(V("PF", 0, 4), V("PI", 0, 4))
+    TT(M("XE"), M("XE"), M("X96"), A_.add)
+    TT(M("XO"), M("XO"), M("X96"), A_.add)
+    TS(M("G1"), M("CMG"), PF(1), A_.is_equal)
+    for r in (0, 1, 6, 7, 2, 3, 8, 9, 4, 5, 10, 11):
+        TS(V("SR1", 128 * r, 128 * r + 128), M("XE"), float(r), A_.is_equal)
+        TS(V("SR2", 128 * r, 128 * r + 128), M("XO"), float(r), A_.is_equal)
+    TT(M("CMT"), M("G1"), M("CM1"), A_.mult)
+    for l in range(3):
+        TS(V("Q3", 128 * l, 128 * l + 128), M("XQ"), float(l), A_.is_equal)
+    TS(M("NI"), M("IDN"), -1.0, A_.mult)
+    for i in range(16):
+        TS(L(i), M("CMT"), float(i + 1), A_.is_equal, 8.0, A_.mult)
+    TS(M("GP"), M("G1"), PF(2), A_.mult)
+
+    p96 = (0, 96)
+    CP(V("F1", 0, 256, 1, p96), V("KR", 0, 256, 1, p96))
+    TT(V("F2", 0, 256, 1, p96), V("KR", 0, 256, 1, p96), V("F1", 0, 256, 1, p96), A_.subtract)
+    for l in range(3):
+        for side in range(2):
+            bank = "B%d" % (2 * l + side)
+            for half in range(2):
+                r = 6 * side + 2 * l + half
+                MM(V(bank, 256 * half, 256 * half + 256),
+                   [(V("SR1", 128 * r, 128 * r + 128, 1, p96), V("F1", 0, 256, 1, p96)),
+                    (V("SR2", 128 * r, 128 * r + 128, 1, p96), V("F2", 0, 256, 1, p96))])
+            c = 1024 * l + 512 * side
+            if side == 0:
+                ACT(V("K", c, c + 512), V(bank, 0, 512))
+            else:
+                CP(V("K", c, c + 512), V(bank, 0, 512))
+        if l == 0:
+            CP(V("MRB", 0, 512, 1, (0, 24)), V("MR", 0, 512, 1, (0, 24)))
+        diag(V("B6", 64 * l, 64 * l + 64), "K", 1024 * l, 1024 * l + 1024)
+        TS(V("KWU", 64 * l, 64 * l + 64), V("B6", 64 * l, 64 * l + 64), 1.0 / 64, A_.mult)
+        MM(V("B7", 0, 512), [(V("Q3", 128 * l, 128 * l + 128, 1, (0, 24)), V("MRB", 0, 512, 1, (0, 24)))])
+        TS(V("SGN", SOFF[l], SOFF[l] + 512), V("B7", 0, 512), 2.0, A_.mult, -1.0, A_.add)
+        if l == 2:
+            TS(V("SC0", 0, 512), V("B7", 0, 512), 255.0, A_.mult, 1.0, A_.add)
+
+    KAB, CAB = w(64), w(64)
+    KD, CD = w(), w()
+    JW = V("JW", 0, 32)
+    NN, G5 = w(64), w(64)
+
+    def top_tables(bank, a):
+        TS(KAB, V(bank, a, a + 64), 1.0 / 64, A_.mult)
+        TS(NN, KAB, float(-NODE0), A_.add, 0.0, A_.max)
+        TS(G5, NN, 512.0, A_.is_ge, 512.0, A_.mult)
+        TT(KD, sub(KAB, 32, 64), sub(KAB, 0, 32), A_.subtract)
+        TT(CAB, NN, G5, A_.add)
+        TT(CD, sub(CAB, 32, 64), sub(CAB, 0, 32), A_.subtract)
+
+    def level(l):
+        hi = NODE0 + 512 * l
+        for h in range(2):
+            c = 64 * l + 16 * h
+            ACT(V("GA", 256 * h, 256 * h + 256), IND(V("Y", 0, hi), V("KWU", c, c + 16)))
+            TT(V("NB", 256 * h, 256 * h + 256), IND(V("Y", 0, hi), V("KWU", c + 32, c + 48)),
+               V("SGN", SOFF[l] + 256 * h, SOFF[l] + 256 * h + 256), A_.mult)
+        for h in range(2):
+            s = (256 * h, 256 * h + 256)
+            TS(V("RB", *s), V("NB", *s), 0.0, A_.min)
+            MM(V("B%d" % h, 0, 256), [(M("IDN"), V("GA", *s)), (M("NI"), V("RB", *s))])
+        for h in range(2):
+            s = (256 * h, 256 * h + 256)
+            TT(V("VV", *s), V("B%d" % h, 0, 256), V("NB", *s), A_.max)
+        for h in range(2):
+            s = (256 * h, 256 * h + 256)
+            TS(V("Y", hi + s[0], hi + s[1]), V("VV", *s), 255.0, A_.min)
+
+    def kid_errors(D, tp, win, a0):
+        f = (0, 512)
+        TS(V("RB", *f), V("NB", *f), 0.0, A_.max)
+        MM(V("B0", *f), tp + [(M("IDN"), V("NB", *f)), (M("N256"), V("RB", *f))])
+        TT(V("XM", *f), V("B4", *f), V("GA", *f), A_.mult)
+        MM(V("B1", *f), tp + [(M("NI"), V("GA", *f)), (M("N254"), V("XM", *f))])
+        wa, wb = V(win, a0, a0 + 512), V(win, a0 + 512, a0 + 1024)
+        TT(V("TMA", *f), V("B0", *f), D, A_.min)
+        TS(wa, V("TMA", *f), 0.0, A_.max)
+        MM(V("B2", *f), [(M("NI"), V("GA", *f)), (M("IDN"), wa)])
+        TT(V("TMB", *f), V("B1", *f), D, A_.min)
+        ACT(V("AB", 0, 512), V("B2", *f), F_.Abs)
+        TS(wb, V("TMB", *f), 0.0, A_.max)
+        MM(V("B3", *f), [(M("N2"), V("RB", *f)), (M("IDN"), V("NB", *f)), (M("IDN"), wb)])
+        ACT(V("AB", 512, 1024), V("B3", *f), F_.Abs)
+        diag(V("B5", 0, 64), "AB", 0, 1024)
+
+    level(0)
+    for nm, c in (("HI", 0.5), ("N256", -256.0), ("N254", -254.0), ("N2", -2.0), ("I255", 255.0)):
+        TS(M(nm), M("IDN"), c, A_.mult)
+    for i in range(16):
+        SEL(V("LP", 128 * i, 128 * i + 128), M("GP"), [[0, 8], [1, 16]], -i, 0)
+    IOTA(JW, [[16, 32]], 0, 0)
+    IOTA(V("KC", 0, 4), [[16, 4]], 0, 0)
+    IOTA(V("DM", 0, 64), [[0, 4], [1, 16]], 0, 0)
+    IOTA(V("K1R", 0, 64), [[1, 64]], 1, 0)
+    IOTA(V("KR0", 0, 64), [[1, 64]], 0, 0)
+    IOTA(M("KT"), [[16, 4], [0, 32]], 0, 0)
+    IOTA(V("MT", 0, 256), [[1, 8], [0, 32]], 0, 0)
+    TT(V("T1", 0, 512), V("D0", 0, 512), V("SC0", 0, 512), A_.mult)
+    level(1)
+    top_tables("B6", 128)
+    TS(M("NG"), M("G1"), -1.0, A_.mult)
+    CP(M("G1F"), M("G1"))
+    TS(M("GL"), M("CM1"), PF(2), A_.is_gt)
+    TT(M("GL"), M("GL"), M("G1"), A_.mult)
+    TS(JW, JW, PF(2), A_.add)
+    TS(V("KC", 0, 4), V("KC", 0, 4), PF(2), A_.add)
+    TS(V("KJ", 0, 4), V("KC", 0, 4), 3072.0, A_.add)
+    TS(V("DM", 0, 64), V("DM", 0, 64), PF(2), A_.is_equal)
+    TS(M("KT"), M("KT"), PF(2), A_.add)
+    TS(PF(4), PF(2), 0.0, A_.is_equal)
+    TS(V("KR0", 0, 64), V("KR0", 0, 64), PF(4), A_.mult)
+    CP(V("CW", 0, 2), V("WTI", 0, 2))
+    FILL(V("YC", 512, 528), -1.0)
+    FILL(V("PM", 0, 48), -1.0)
+    FILL(V("KEYW", 0, 48), 0.0)
+    FILL(V("DONW", 0, 48), 0.0)
+    TS(V("KOL", 0, 8), V("G1", 0, 128, 16), 0.125, A_.mult)
+
+    base = wtop[0]
+    CC = w(4)
+    EW, TB1, EM1, T5, DL, M1, COL, C1, LIVE, LV5, P5 = w(64), w(), w(), w(), w(), w(), w(), w(), w(), w(), w()
+    K2F, EW2, TB2, EM2, X1, X2, X3, DL2, E8, KY1, KY2 = w(64), w(64), w(), w(), w(), w(), w(), w(), w(), w(), w()
+    US, S1, S2, S4, CD8, RUN, BEST = w(64), w(), w(64), w(128), w(256), w(64), w()
+    SW, BI1, BI2, A1, A2, O1, O2, O3, VA = w(4), w(4), w(4), w(4), w(4), w(4), w(4), w(4), w(4)
+    I0, I1, I2, I3, I4, I5 = [V("WI", 32 * k, 32 * k + 32) for k in range(6)]
+    f = (0, 512)
+
+    for t in range(3):
+        MM(V("B4", *f), [(M("HI"), V("SGN", SOFF[2], SOFF[2] + 512)), (M("HI"), V("ONE", *f))])
+        ACT(V("GA", *f), IND(V("Y", 0, 3328), V("KWU", 128, 160)))
+        TT(V("NB", *f), IND(V("Y", 0, 3328), V("KWU", 160, 192)), V("SGN", SOFF[2], SOFF[2] + 512), A_.mult)
+        kid_errors(V("D0", *f), [(M("IDN"), V("T1", *f))], "WIN", 0)
+        CP(EW, V("B5", 0, 64))
+        TT(TB1, sub(EW, 32, 64), sub(EW, 0, 32), A_.is_lt)
+        TT(M1, TB1, CD, A_.mult)
+        TT(COL, M1, sub(CAB, 0, 32), A_.add)
+        CP(V("LU", 0, 32), COL)
+        CP(V("FF", 0, 512), IND(V("K", 0, 1536), V("LU", 0, 32)))
+        ACT(V("FF", 512, 1024), IND(V("K", 512, 2048), V("LU", 0, 32)))
+        ACT(V("SG2", *f), IND(V("SGN", 0, 1536), V("LU", 0, 32)))
+        diag(V("B6", 0, 64), "FF", 0, 1024)
+        MM(V("B4", *f), [(M("HI"), V("ONE", *f)), (M("HI"), V("SG2", *f))])
+        TS(T5, TB1, 512.0, A_.mult)
+        TT(DL, T5, JW, A_.add)
+        CP(V("DLU", 0, 32), DL)
+        ACT(V("WIN2", *f), IND(V("WIN", 0, 1024), V("DLU", 0, 32)))
+        TT(M1, TB1, KD, A_.mult)
+        TT(C1, M1, sub(KAB, 0, 32), A_.add)
+        TS(V("K2U", 0, 64), V("B6", 0, 64), 1.0 / 64, A_.mult)
+        ACT(V("GA", *f), IND(V("Y", 0, 2816), V("K2U", 0, 32)))
+        TT(V("NB", *f), IND(V("Y", 0, 2816), V("K2U", 32, 64)), V("SG2", *f), A_.mult)
+        TT(V("MD", *f), V("B4", *f), V("WIN2", *f), A_.mult)
+        TT(EM1, sub(EW, 32, 64), sub(EW, 0, 32), A_.min)
+        TS(LIVE, C1, float(NODE0), A_.is_ge)
+        TS(K2F, V("B6", 0, 64), 1.0 / 64, A_.mult)
+        TS(LV5, LIVE, 512.0, A_.mult)
+        TT(P5, LV5, JW, A_.add)
+        kid_errors(V("WIN2", *f), [(M("IDN"), V("WIN2", *f)), (M("I255"), V("MD", *f))], "WIN2", 512)
+        TT(KD if t > 5 else X3, sub(K2F, 32, 64), sub(K2F, 0, 32), A_.subtract)
+        CP(EW2, V("B5", 0, 64))
+        TT(TB2, sub(EW2, 32, 64), sub(EW2, 0, 32), A_.is_lt)
+        TT(X1, TB2, LV5, A_.mult)
+        TT(DL2, X1, P5, A_.add)
+        CP(V("LU", 32, 64), DL2)
+        ACT(V("DC", 0, 512), IND(V("WIN2", 0, 1536), V("LU", 32, 64)), F_.Copy, None, V("CW", 0, 1))
+        CP(V("DN", *f), IND(V("WIN2", 0, 1536), V("LU", 32, 64)))
+        TS(V("DC", 512, 1024), V("DN", *f), V("CW", 1, 2), A_.mult)
+        diag(V("B7", 0, 64), "DC", 0, 1024)
+        TT(EM2, sub(EW2, 32, 64), sub(EW2, 0, 32), A_.min)
+        TT(X3, X3, TB2, A_.mult)
+        TT(EM2, EM2, EM1, A_.subtract)
+        TT(X3, X3, sub(K2F, 0, 32), A_.add)
+        TT(EM2, EM2, LIVE, A_.mult)
+        TT(X3, X3, C1, A_.subtract)
+        TT(E8, EM2, EM1, A_.add)
+        TT(X3, X3, LIVE, A_.mult)
+        TS(US, V("B7", 0, 64), 0.125, A_.mult)
+        U1, U2 = sub(US, 0, 32), sub(US, 32, 64)
+        TT(I0, U1, U2, A_.mult)
+        CP(I3, U1)
+        TS(I1, I0, 5, A_.arith_shift_right)
+        TS(I4, I3, 127, A_.bitwise_and)
+        TT(I2, I1, U2, A_.add)
+        TS(S1, I4, 2.0, A_.mult, 1.0, A_.add)
+        TS(I5, I2, 2047, A_.bitwise_and)
+        TS(sub(S2, 0, 32), I4, 4.0, A_.mult, 2.0, A_.add)
+        CP(V("CU", 0, 32), I5)
+        ACT(V("CG", 0, 512), IND(V("LIBW", 0, 3840), V("CU", 0, 32)))
+        CP(sub(CD8, 0, 32), I5)
+        TS(sub(S2, 32, 64), I4, 4.0, A_.mult, 2.0, A_.add)
+        TT(sub(CD8, 32, 64), sub(CD8, 0, 32), S1, A_.add)
+        CP(V("CU", 32, 64), sub(CD8, 32, 64))
+        ACT(V("CG", 512, 1024), IND(V("LIBW", 0, 3840), V("CU", 32, 64)))
+        TT(sub(CD8, 64, 128), sub(CD8, 0, 64), S2, A_.add)
+        CP(V("CU", 64, 128), sub(CD8, 64, 128))
+        for h in range(2):
+            s = (512 * h, 512 * h + 512)
+            TT(V("XA0", *s), IND(V("LIBW", 0, 3840), V("CU", 64 + 32 * h, 96 + 32 * h)), V("DN", *f), A_.subtract)
+            MM(V("B%d" % (2 + h), *f), [(M("NI"), V("DN", *f)), (M("IDN"), V("CG", *s))])
+        for h in range(2):
+            ACT(V("AC0", 512 * h, 512 * h + 512), V("B%d" % (2 + h), *f), F_.Abs)
+        diag(V("B5", 0, 64), "AC0", 0, 1024, [(M("IDN"), V("MT", 0, 64))])
+        for h in range(2):
+            TS(sub(S4, 64 * h, 64 * h + 64), S2, 2.0, A_.mult)
+        TT(sub(CD8, 128, 256), sub(CD8, 0, 128), S4, A_.add)
+        CP(V("CU", 128, 256), sub(CD8, 128, 256))
+        ACT(V("AC1", 0, 1024), V("XA0", 0, 1024), F_.Abs)
+        diag(V("B6", 0, 64), "AC1", 0, 1024, [(M("IDN"), V("MT", 64, 128))])
+        for h in range(2):
+            TT(V("XA1", 512 * h, 512 * h + 512), IND(V("LIBW", 0, 3840), V("CU", 128 + 32 * h, 160 + 32 * h)), V("DN", *f), A_.subtract)
+        ACT(V("AC0", 0, 1024), V("XA1", 0, 1024), F_.Abs)
+        TT(X3, X3, C1, A_.add)
+        CP(V("CHU", 0, 32), X3)
+        CP(RUN, V("B5", 0, 64))
+        diag(V("B5", 0, 64), "AC0", 0, 1024, [(M("IDN"), V("MT", 128, 192))])
+        for h in range(2):
+            s = (512 * h, 512 * h + 512)
+            TT(V("XA2", *s), IND(V("LIBW", 0, 3840), V("CU", 192 + 32 * h, 224 + 32 * h)), V("DN", *f), A_.subtract)
+            ACT(V("AC1", *s), V("XA2", *s), F_.Abs)
+            if h == 0:
+                TT(RUN, V("B6", 0, 64), RUN, A_.min)
+        diag(V("B6", 0, 64), "AC1", 0, 1024, [(M("IDN"), V("MT", 192, 256))])
+        ACT(V("YC", *f), IND(V("Y", 0, 3840), V("CHU", 0, 32)))
+        TT(RUN, V("B5", 0, 64), RUN, A_.min)
+        TT(RUN, V("B6", 0, 64), RUN, A_.min)
+        TT(BEST, sub(RUN, 0, 32), sub(RUN, 32, 64), A_.min)
+        TT(V("BB", 0, 32), BEST, E8, A_.is_lt)
+        op("v", [("ONE", 0, 32), ("BB", 0, 32)], [("INC", 0, 32)],
+           lambda: g.vector.tensor_tensor_scan(T.INC[:, 0:32], T.ONE[:, 0:32], T.BB[:, 0:32], 0.0, A_.mult, A_.add))
+        for q in range(4):
+            MM(V("B0", 32 * q, 32 * q + 32), [(M("G1"), V("INC", 0, 32))])
+        MM(V("B1", 0, 32), [(M("G1"), V("INC", 0, 32)), (M("NG"), V("BB", 0, 32)), (M("GL"), V("BB", 0, 32))])
+        TT(M("CMP"), V("B0", 0, 128), M("KT"), A_.is_le)
+        TT(V("PM", 0, 32), V("B1", 0, 32), V("BB", 0, 32), A_.mult)
+        for q in range(4):
+            RED(sub(CC, q, q + 1), V("CMP", 32 * q, 32 * q + 32))
+        CP(V("CCU", 0, 4), CC)
+        TS(V("CC16", 0, 4), CC, 16.0, A_.mult)
+        TT(V("OH", 0, 64), IND(V("PM", 0, 48), V("CCU", 0, 4)), V("K1R", 0, 64), A_.is_equal)
+        MM(V("B2", 0, 4), [(M("IDN"), V("CC16", 0, 4))] + [(V("LP", 128 * i, 128 * i + 128), V("OH", i, 64, 16)) for i in range(16)])
+        CP(V("JLU", 0, 4), V("B2", 0, 4))
+        SND = "SND%d" % t
+        CP(V(SND, 0, 64), IND(V("YC", 0, 528), V("JLU", 0, 4)))
+        waits("g", [(SND, 0, 64)], [])
+        land = "LAND%d" % t if hop is None else "RLY%d" % t
+        g.remote_dma(T[land][:], T[SND][:], T.sem[("arr%d" if hop is None else "hop%d") % t], T.sem["snt%d" % t], spid, srid, smask)
+        TS(KY1, DL, 2048.0, A_.add)
+        TS(KY2, TB2, 512.0, A_.mult)
+        CP(I0, BEST)
+        TT(KY2, KY2, COL, A_.add)
+        TS(I1, I0, 7, A_.bitwise_and)
+        TT(KY2, KY2, KY1, A_.subtract)
+        TT(X1, I1, S1, A_.mult)
+        TT(KY2, KY2, LIVE, A_.mult)
+        TT(X1, X1, sub(CD8, 0, 32), A_.add)
+        TT(KY2, KY2, KY1, A_.add)
+        TS(X2, X1, 2048.0, A_.is_ge, 2048.0, A_.mult)
+        TS(V("KEYW", 0, 32), KY2, 128.0, A_.mult)
+        TT(V("DONW", 0, 32), X1, X2, A_.subtract)
+        TT(V("VK", 0, 64), IND(V("KEYW", 0, 48), V("CCU", 0, 4)), V("OH", 0, 64), A_.mult)
+        TT(V("VD", 0, 64), IND(V("DONW", 0, 48), V("CCU", 0, 4)), V("OH", 0, 64), A_.mult)
+        MM(V("B3", 0, 64), [(M("G1F"), V("VK", 0, 64)), (M("G1F"), V("KR0", 0, 64))])
+        MM(V("B7", 0, 64), [(M("G1F"), V("VD", 0, 64))])
+        TT(V("SWT", 0, 64), V("B3", 0, 64), V("DM", 0, 64), A_.mult)
+        for q in range(4):
+            RED(sub(SW, q, q + 1), V("SWT", 16 * q, 16 * q + 16))
+        TS(BI1, SW, -0.5, A_.add)
+        TS(BI2, SW, -63.5, A_.add)
+        for q in range(4):
+            ACT(V("SGJ", 0, 64), V("B3", 0, 64), F_.Sign, sub(BI1, q, q + 1), -1.0, sub(A1, q, q + 1))
+            ACT(V("SGJ", 0, 64), V("B3", 0, 64), F_.Sign, sub(BI2, q, q + 1), -1.0, sub(A2, q, q + 1))
+        TS(V("TQ", 0, 64), V("B7", 0, 64), PF(3), A_.mult)
+        TS(VA, CC, 32.0, A_.is_lt)
+        TS(O1, SW, 1.0 / 128, A_.mult, -3072.0, A_.add)
+        TT(V("SRC", 0, 64), V("B7", 0, 64), V("TQ", 0, 64), A_.subtract)
+        TS(O2, V("KC", 0, 4), 129.0 / 128, A_.mult)
+        TT(O1, O1, O2, A_.subtract)
+        TT(O1, O1, VA, A_.mult)
+        TT(O3, A1, A2, A_.subtract)
+        TS(O3, O3, 1.0, A_.is_lt)
+        TT(O1, O1, O3, A_.mult)
+        TT(O1, O1, V("KJ", 0, 4), A_.add)
+        CP(V("OFU", 0, 4), O1)
+        op("v", [("SRC", 0, 64), ("OFU", 0, 4)], [("K", 0, 3136)],
+           lambda: g.vector.tensor_copy(out=T.K[:, 0:3136].indirect(T.OFU[:, 0:4]), in_=T.SRC[:, 0:64]))
+        for l in range(3):
+            diag(V("B4", 64 * l, 64 * l + 64), "K", 1024 * l, 1024 * l + 1024)
+        TS(V("KWU", 0, 192), V("B4", 0, 192), 1.0 / 64, A_.mult)
+        if t < 2:
+            top_tables("B4", 128)
+        else:
+            for l in range(3):
+                for side in range(2):
+                    c = 1024 * l + 512 * side
+                    bank = "B%d" % (5 + side)
+                    p8 = (0, 8)
+                    MM(V(bank, 0, 512, 1, p8), [(V("KOL", 0, 8), V("K", c, c + 512))])
+                    o = 1536 * side + 512 * l
+                    ACT(V("KOB", o, o + 512, 1, p8), V(bank, 0, 512, 1, p8))
+            waits("s", [("KOB", 0, 3072)], [])
+            DMA("s", T.ko[:], T.KOB[0:8, :], [("KOB", 0, 3072)], [])
+        a = 64 * t
+        g.vector.wait_ge(T.sem["arr%d" % t], acnt)
+        lnd = V("LAND%d" % t, 0, 64)
+        TS(V("MGM", 0, 64), lnd, 0.0, A_.is_lt)
+        TT(V("MGO", 0, 64), V("Y", a, a + 64), V("MGM", 0, 64), A_.mult)
+        TT(V("Y", a, a + 64), lnd, V("MGO", 0, 64), A_.max)
+        if t == 2:
+            DMA("s", T.yo[:, 0:NODE0], T.Y[:, 0:NODE0], [("Y", 0, NODE0)], [])
+        level(0)
+        if t < 2:
+            CP(V("LIBW", a, a + 64), V("Y", a, a + 64))
+            CP(V("LIBW", LIB + a, LIB + a + 64), V("Y", a, a + 64))
+        else:
+            DMA("s", T.yo[:, NODE0:NODE0 + 512], T.Y[:, NODE0:NODE0 + 512], [("Y", NODE0, NODE0 + 512)], [])
+        level(1)
+        if t == 2:
+            DMA("s", T.yo[:, 2816:3328], T.Y[:, 2816:3328], [("Y", 2816, 3328)], [])
+            level(2)
+            DMA("s", T.yo[:, 3328:3840], T.Y[:, 3328:3840], [("Y", 3328, 3840)], [])
+
+    for t in range(3):
+        g.wait_ge(T.sem["snt%d" % t], scnt)
+    for k in range(nd[0]):
+        g.sync.wait_ge(T.sem["d%d" % k], 16)
+    for q in ("v", "a", "p", "g"):
+        g.sync.wait_ge(T.sem["q" + q], cnt[q])

@@ -1,34 +1,21 @@
-from concourse.bass import DstId, RemoteDMATransfer
-from concourse.mybir import dt, AluOpType, AxisListType, ActivationFunctionType
+from concourse.mybir import AluOpType, AxisListType, ActivationFunctionType
 
 A_ = AluOpType
 F_ = ActivationFunctionType
 
 SCRATCH = {}
-for _n, _w, _t in (
-        ("Y", 3840, "bfloat16"), ("LIBW", 3840, "bfloat16"), ("K", 3136, "bfloat16"), ("KR", 256, "int32"), ("F1", 256, "bfloat16"),
-        ("F2", 256, "bfloat16"), ("MR", 512, "int32"), ("MRB", 512, "bfloat16"), ("SGN", 1536, "bfloat16"), ("D0", 512, "bfloat16"),
-        ("SC0", 512, "bfloat16"), ("T1", 512, "bfloat16"), ("WTI", 2, "int32"), ("CW", 2, "float32"),
-        ("ONE", 512, "bfloat16"), ("IDN", 128, "bfloat16"), ("NI", 128, "bfloat16"), ("HI", 128, "bfloat16"), ("I255", 128, "bfloat16"),
-        ("N256", 128, "bfloat16"), ("N254", 128, "bfloat16"), ("N2", 128, "bfloat16"), ("CMG", 128, "bfloat16"), ("CM1", 128, "bfloat16"),
-        ("G1", 128, "bfloat16"), ("NG", 128, "bfloat16"), ("G1F", 128, "float32"), ("GL", 128, "bfloat16"), ("GP", 128, "bfloat16"),
-        ("CMT", 128, "bfloat16"), ("L8", 2048, "bfloat16"), ("LP", 2048, "bfloat16"), ("X96", 128, "bfloat16"), ("SR1", 1536, "bfloat16"),
-        ("PAR", 128, "bfloat16"), ("XE", 128, "bfloat16"), ("XO", 128, "bfloat16"),
-        ("SR2", 1536, "bfloat16"), ("XQ", 128, "bfloat16"), ("Q3", 384, "bfloat16"), ("KOL", 8, "bfloat16"), ("PI", 8, "int32"), ("PF", 8, "float32"),
-        ("KT", 128, "bfloat16"), ("K1R", 64, "bfloat16"), ("KR0", 64, "float32"), ("DM", 64, "float32"), ("JW", 32, "float32"),
-        ("MT", 256, "bfloat16"), ("KC", 4, "float32"), ("KJ", 4, "float32"),
-        ("GA", 512, "bfloat16"), ("NB", 512, "bfloat16"), ("RB", 512, "bfloat16"), ("VV", 512, "bfloat16"), ("XM", 512, "bfloat16"),
-        ("MD", 512, "bfloat16"), ("TMA", 512, "bfloat16"), ("TMB", 512, "bfloat16"), ("WIN", 1024, "bfloat16"), ("WIN2", 1536, "bfloat16"),
-        ("AB", 1024, "bfloat16"), ("FF", 1024, "bfloat16"), ("SG2", 512, "bfloat16"), ("DN", 512, "bfloat16"), ("DC", 1024, "bfloat16"),
-        ("CG", 1024, "bfloat16"), ("XA0", 1024, "bfloat16"), ("XA1", 1024, "bfloat16"), ("XA2", 1024, "bfloat16"),
-        ("AC0", 1024, "bfloat16"), ("AC1", 1024, "bfloat16"), ("YC", 528, "bfloat16"),
-        ("WR", 2048, "float32"), ("WI", 256, "int32"), ("KWU", 192, "uint16"), ("LU", 64, "uint16"), ("K2U", 64, "uint16"), ("DLU", 32, "uint16"),
-        ("CHU", 32, "uint16"), ("CU", 256, "uint16"), ("CCU", 4, "uint16"), ("JLU", 4, "uint16"), ("OFU", 4, "uint16"),
-        ("BB", 32, "bfloat16"), ("INC", 32, "bfloat16"), ("CMP", 128, "bfloat16"), ("CC16", 4, "bfloat16"), ("PM", 48, "float32"),
-        ("OH", 64, "bfloat16"), ("KEYW", 48, "float32"), ("DONW", 48, "float32"), ("VK", 64, "float32"), ("VD", 64, "float32"),
-        ("SWT", 64, "float32"), ("SGJ", 64, "float32"), ("TQ", 64, "bfloat16"), ("SRC", 64, "bfloat16"), ("MGM", 64, "bfloat16"),
-        ("MGO", 64, "bfloat16"), ("KOB", 3072, "float32")):
-    SCRATCH[_n] = ("sbuf", [128, _w], _t)
+for _t, _s in (
+        ("bfloat16", "Y 3840 LIBW 3840 K 3136 F1 256 F2 256 MRB 512 SGN 1536 D0 512 MD0 512 ONE 512 IDN 128 NI 128 I128 128 I255 128 N256 128 "
+                     "N254 128 N2 128 CMG 128 CM1 128 G1 128 NG 128 GL 128 GP 128 CMT 128 L8 2048 LP 2048 X96 128 SR1 1536 PAR 128 XE 128 XO 128 "
+                     "SR2 1536 XQ 128 Q3 384 KOL 8 KT 128 K1R 64 MT 256 GA 512 NB 512 RB 512 VV 512 XM 512 MD 512 TMA 512 TMB 512 WIN 1024 "
+                     "WIN2 1536 AB 1024 FFA 1024 FFB 1024 SG2 512 DN 512 DC 1024 CG 1024 XA0 1024 XA1 1024 XA2 1024 AC0 1024 AC1 1024 AC2 1024 "
+                     "AC3 1024 YC 528 BB 32 INC 32 CMP 128 CC16 4 OH 64 TQ 64 SRC 64 MGM 64 MGO 64"),
+        ("float32", "CW 2 PF 8 G1F 128 KR0 64 DM 64 JW 32 KC 4 KJ 4 KC2 4 WR 2560 PM 48 KEYW 48 DONW 48 VK 64 VD 64 ROWS 64 SWT 64 SGJ 64 CMQ 256 KOB 3072"),
+        ("int32", "KR 256 MR 512 WTI 2 PI 8 WI 256"),
+        ("uint16", "KWU 192 CABU 64 LU 64 K2U 64 DLU 32 CHU 32 CU 256 CCU 4 JLU 4 OFU 4")):
+    _w = _s.split()
+    for _k in range(0, len(_w), 2):
+        SCRATCH[_w[_k]] = ("sbuf", [128, int(_w[_k + 1])], _t)
 for _k in range(3):
     for _n in ("SND", "LAND", "RLY"):
         SCRATCH["%s%d" % (_n, _k)] = ("sbuf", [128, 64], "bfloat16")
@@ -37,7 +24,7 @@ for _k in range(8):
 
 SEMAPHORES = ["qv", "qa", "qp", "qg"] + ["d%d" % k for k in range(20)] + ["%s%d" % (n, k) for n in ("hop", "arr", "snt", "rst") for k in range(3)]
 
-LIB, LEAF, MN, NODE0 = 2048, 256, 512, 2304
+LIB, NODE0 = 2048, 2304
 SOFF = (0, 1024, 512)
 
 
@@ -90,6 +77,7 @@ def rank_program(g, core, T, topo):
     clock = {"v": {}, "a": {}, "p": {}, "g": {}, "s": {}}
     acc = {}
     nd = [0]
+    seq = [0]
 
     def waits(q, reads, writes):
         need = []
@@ -97,13 +85,11 @@ def rank_program(g, core, T, topo):
             for nm, a, b in lst:
                 ps = nm[0] == "B" and nm[1:].isdigit()
                 for e in acc.get(nm, ()):
-                    if not ps and (e[1] <= a or e[0] >= b):
+                    apart = e[1] <= a or e[0] >= b
+                    if apart and (not ps or e[3] == q):
                         continue
                     if e[2] or wr or (ps and e[3] != q):
-                        if e[3] == q and q != "s" and (wr or (q == "p" and wr)):
-                            if not (e[2] and wr) or q == "p":
-                                continue
-                        if ps and e[3] == q and (e[1] <= a or e[0] >= b):
+                        if e[3] == q and wr and (q == "p" or not e[2]):
                             continue
                         need.append((e[6], e[4], e[5], e[7]))
         need.sort(key=lambda x: -x[0])
@@ -117,10 +103,8 @@ def rank_program(g, core, T, topo):
                     ck[k] = clk[k]
             ck[sem] = max(val, ck.get(sem, 0))
 
-    seq = [0]
-
-    def note(q, reads, writes, sem, val):
-        clk = dict(clock[q])
+    def note(q, clk, reads, writes, sem, val):
+        clk = dict(clk)
         clk[sem] = val
         seq[0] += 1
         for lst, wr in ((reads, False), (writes, True)):
@@ -137,7 +121,7 @@ def rank_program(g, core, T, topo):
         waits(q, reads, writes)
         cnt[q] += 1
         f().then_inc(T.sem["q" + q], 1)
-        note(q, reads, writes, "q" + q, cnt[q])
+        note(q, clock[q], reads, writes, "q" + q, cnt[q])
 
     def V(nm, a, b, st=1, p=None):
         if p is None:
@@ -154,17 +138,14 @@ def rank_program(g, core, T, topo):
 
     def TS(o, x, s1, f1, s2=None, f2=None):
         rd = list(x[1])
-        a1, a2 = s1, s2
+        a1 = s1
         if isinstance(s1, tuple):
             rd += s1[1]
             a1 = s1[0]
-        if isinstance(s2, tuple):
-            rd += s2[1]
-            a2 = s2[0]
         if f2 is None:
             op("v", rd, o[1], lambda: g.vector.tensor_scalar(out=o[0], in0=x[0], scalar1=a1, scalar2=None, op0=f1))
         else:
-            op("v", rd, o[1], lambda: g.vector.tensor_scalar(out=o[0], in0=x[0], scalar1=a1, scalar2=a2, op0=f1, op1=f2))
+            op("v", rd, o[1], lambda: g.vector.tensor_scalar(out=o[0], in0=x[0], scalar1=a1, scalar2=s2, op0=f1, op1=f2))
 
     def CP(o, x):
         op("v", x[1], o[1], lambda: g.vector.tensor_copy(out=o[0], in_=x[0]))
@@ -177,30 +158,24 @@ def rank_program(g, core, T, topo):
 
     def ACT(o, x, f=F_.Copy, bias=None, scale=None, accum=None):
         rd, wr, kw = list(x[1]), list(o[1]), {}
-        if bias is not None:
-            rd += bias[1]
-            kw["bias"] = bias[0]
-        if scale is not None:
-            if isinstance(scale, tuple):
-                rd += scale[1]
-                kw["scale"] = scale[0]
-            else:
-                kw["scale"] = scale
+        for nm, c in (("bias", bias), ("scale", scale)):
+            if isinstance(c, tuple):
+                rd += c[1]
+                kw[nm] = c[0]
+            elif c is not None:
+                kw[nm] = c
         if accum is not None:
             wr += accum[1]
             kw["accum_out"] = accum[0]
         op("a", rd, wr, lambda: g.scalar.activation(out=o[0], in_=x[0], func=f, **kw))
 
+    def mm(o, l, r, start, stop):
+        op("p", l[1] + r[1], o[1], lambda: g.tensor.matmul(o[0], l[0], r[0], start, stop))
+
     def MM(o, prs):
-        rd = []
-        for l, r in prs:
-            rd += l[1] + r[1]
-        def f():
-            ins = None
-            for k in range(len(prs)):
-                ins = g.tensor.matmul(o[0], prs[k][0][0], prs[k][1][0], k == 0, k == len(prs) - 1)
-            return ins
-        op("p", rd, o[1], f)
+        n = len(prs)
+        for k in range(n):
+            mm(o, prs[k][0], prs[k][1], k == 0, k == n - 1)
 
     def IOTA(o, pat, base, ch):
         op("g", [], o[1], lambda: g.iota(o[0], pat, base, ch, allow_small_or_imprecise_dtypes=True))
@@ -213,13 +188,10 @@ def rank_program(g, core, T, topo):
         nd[0] += 1
         waits(q, reads, writes)
         eng[q].dma_start(out=o, in_=x).then_inc(T.sem[sem], 16)
-        note("dma" + sem, reads, writes, sem, 16)
+        note("dma" + sem, {}, reads, writes, sem, 16)
 
-    for k in range(20):
-        clock["dmad%d" % k] = {}
-
-    def M(nm, p=None):
-        return V(nm, 0, 128, 1, p)
+    def M(nm):
+        return V(nm, 0, 128)
 
     wtop = [0]
 
@@ -236,7 +208,87 @@ def rank_program(g, core, T, topo):
         return V("L8", 128 * i, 128 * i + 128)
 
     def diag(out, nm, lo, hi, more=()):
-        MM(out, [(L(i), V(nm, lo + i, hi, 16)) for i in range(16)] + list(more))
+        MM(out, list(more) + [(L(i), V(nm, lo + i, hi, 16)) for i in range(16)])
+
+    f = (0, 512)
+    PI = lambda k: V("PI", k, k + 1)
+    PF = lambda k: V("PF", k, k + 1)
+    JW = V("JW", 0, 32)
+    KAB, CAB, NN, G5, KD, CD = w(64), w(64), w(64), w(64), w(), w()
+    GKF, GKD = w(128), w(64)
+
+    def kid_lists(l, bank):
+        diag(V(bank, 64 * l, 64 * l + 64), "K", 1024 * l, 1024 * l + 1024)
+        TS(V("KWU", 64 * l, 64 * l + 64), V(bank, 64 * l, 64 * l + 64), 1.0 / 64, A_.mult)
+
+    def top_tables(bank):
+        TS(KAB, V(bank, 128, 192), 1.0 / 64, A_.mult)
+        TS(NN, KAB, float(-NODE0), A_.add, 0.0, A_.max)
+        TS(G5, NN, 512.0, A_.is_ge, 512.0, A_.mult)
+        TT(CAB, NN, G5, A_.add)
+        CP(V("CABU", 0, 64), CAB)
+
+    def grandkids(k):
+        off = V("CABU", 32 * (k // 2), 32 * (k // 2) + 32)
+        o = V("FFA" if k < 2 else "FFB", 512 * (k % 2), 512 * (k % 2) + 512)
+        win = V("K", 512 * (k % 2), 1536 + 512 * (k % 2))
+        if k < 3:
+            ACT(o, IND(win, off))
+        else:
+            CP(o, IND(win, off))
+
+    def level(l, mid=None):
+        hi = NODE0 + 512 * l
+        hs = [(256 * h, 256 * h + 256) for h in range(2)]
+        for h in range(2):
+            c = 64 * l + 16 * h
+            ACT(V("GA", *hs[h]), IND(V("Y", 0, hi), V("KWU", c, c + 16)))
+            TT(V("NB", *hs[h]), IND(V("Y", 0, hi), V("KWU", c + 32, c + 48)), V("SGN", SOFF[l] + 256 * h, SOFF[l] + 256 * h + 256), A_.mult)
+        if mid is not None:
+            mid()
+        for h in range(2):
+            TS(V("RB", *hs[h]), V("NB", *hs[h]), 0.0, A_.min)
+            MM(V("B%d" % h, 0, 256), [(M("IDN"), V("GA", *hs[h])), (M("NI"), V("RB", *hs[h]))])
+        for h in range(2):
+            TT(V("VV", *hs[h]), V("B%d" % h, 0, 256), V("NB", *hs[h]), A_.max)
+        for h in range(2):
+            TS(V("Y", hi + hs[h][0], hi + hs[h][1]), V("VV", *hs[h]), 255.0, A_.min)
+
+    SCHED1 = ((0, "IDN", "D"), (0, "I255", "MDb"), (1, "IDN", "D"), (1, "I255", "MDb"), (4, "I128", "SG"), (4, "IDN", "GA"),
+              (0, "IDN", "NB"), (0, "N256", "RB"), (1, "NI", "GA"), (1, "N254", "XM"))
+    SCHED2 = ((7, "I128", "SG"), (4, "I128", "SG"), (7, "IDN", "D"), (0, "IDN", "D"), (1, "IDN", "D"), (4, "IDN", "GA"), (1, "NI", "GA"),
+              (0, "IDN", "NB"), (0, "I255", "MDb"), (0, "N256", "RB"), (1, "I255", "MDb"), (1, "N254", "XM"))
+
+    def kid_errors(D, MDb, SG, win, a0, EWA, sched, pre=None, mid=None):
+        src = {"D": D, "MDb": MDb, "SG": SG}
+        left = [e[0] for e in sched]
+        seen = []
+        for o, l, r in sched:
+            if r == "MDb" and o == 0 and 7 in seen:
+                ACT(MDb, V("B7", *f), F_.Relu, -128.0)
+            if r == "RB":
+                TS(V("RB", *f), V("NB", *f), 0.0, A_.max)
+            if r == "XM":
+                ACT(V("XM", *f), V("B4", *f), F_.Relu, -128.0)
+            left.remove(o)
+            mm(V("B%d" % o, *f), M(l), src[r] if r in src else V(r, *f), o not in seen, o not in left)
+            seen.append(o)
+        if pre is not None:
+            pre()
+        wa, wb = V(win, a0, a0 + 512), V(win, a0 + 512, a0 + 1024)
+        TT(V("TMA", *f), V("B0", *f), D, A_.min)
+        TS(wa, V("TMA", *f), 0.0, A_.max)
+        TT(V("TMB", *f), V("B1", *f), D, A_.min)
+        MM(V("B2", *f), [(M("NI"), V("GA", *f)), (M("IDN"), wa)])
+        ACT(V("AB", 0, 512), V("B2", *f), F_.Abs)
+        TS(wb, V("TMB", *f), 0.0, A_.max)
+        MM(V("B3", *f), [(M("N2"), V("RB", *f)), (M("IDN"), V("NB", *f)), (M("IDN"), wb)])
+        diag(V("B5", 0, 32), "AB", 0, 512)
+        ACT(V("AB", 512, 1024), V("B3", *f), F_.Abs)
+        if mid is not None:
+            mid()
+        CP(EWA, V("B5", 0, 32))
+        diag(V("B6", 0, 32), "AB", 512, 1024)
 
     DMA("s", T.KR[0:96, :], T.kid[:], [], [("KR", 0, 256)])
     DMA("a", T.MR[0:24, :], T.mx[:], [], [("MR", 0, 512)])
@@ -246,344 +298,331 @@ def rank_program(g, core, T, topo):
     DMA("s", T.LIBW[:, 0:LIB], T.lv[:, 0:LIB], [], [("LIBW", 0, LIB)])
     DMA("s", T.LIBW[:, LIB:3840], T.lv[:, 0:1792], [], [("LIBW", LIB, 3840)])
 
-    PI = lambda k: V("PI", k, k + 1)
-    PF = lambda k: V("PF", k, k + 1)
     FILL(V("ONE", 0, 512), 1.0)
     op("g", [], PI(0)[1], lambda: g.iota(PI(0)[0], [[0, 1]], 0, 1))
-    IOTA(M("X96"), [[-12, 8], [0, 16]], 0, 1)
     IOTA(M("PAR"), [[0, 64], [1, 2]], 0, 0)
+    IOTA(M("X96"), [[-12, 8], [0, 16]], 0, 1)
     IOTA(M("CMG"), [[1, 8], [0, 16]], 0, 0)
     IOTA(M("CM1"), [[0, 8], [1, 16]], 1, 0)
     IOTA(M("XQ"), [[-3, 8], [0, 16]], 0, 1)
     SEL(M("IDN"), V("ONE", 0, 128), [[-1, 128]], 0, 1)
+    IOTA(JW, [[16, 32]], 0, 0)
+    IOTA(V("KC", 0, 4), [[16, 4]], 0, 0)
+    IOTA(V("DM", 0, 64), [[0, 4], [1, 16]], 0, 0)
+    IOTA(V("KR0", 0, 64), [[1, 64]], 0, 0)
+    IOTA(V("K1R", 0, 64), [[1, 64]], 1, 0)
+    IOTA(M("KT"), [[16, 4], [0, 32]], 0, 0)
+    IOTA(V("MT", 0, 256), [[1, 8], [0, 32]], 0, 0)
     TS(PI(1), PI(0), 4, A_.arith_shift_right)
     TS(PI(2), PI(0), 15, A_.bitwise_and)
     TS(PI(3), PI(0), 1, A_.bitwise_and)
-    TS(V("XE", 0, 128), M("PAR"), 200.0, A_.mult)
-    TS(V("XO", 0, 128), M("PAR"), -200.0, A_.mult, 200.0, A_.add)
+    TS(M("XE"), M("PAR"), 200.0, A_.mult)
+    TS(M("XO"), M("PAR"), -200.0, A_.mult, 200.0, A_.add)
     CP(V("PF", 0, 4), V("PI", 0, 4))
     TT(M("XE"), M("XE"), M("X96"), A_.add)
     TT(M("XO"), M("XO"), M("X96"), A_.add)
     TS(M("G1"), M("CMG"), PF(1), A_.is_equal)
-    for r in (0, 1, 6, 7, 2, 3, 8, 9, 4, 5, 10, 11):
-        TS(V("SR1", 128 * r, 128 * r + 128), M("XE"), float(r), A_.is_equal)
-        TS(V("SR2", 128 * r, 128 * r + 128), M("XO"), float(r), A_.is_equal)
-    TT(M("CMT"), M("G1"), M("CM1"), A_.mult)
-    for l in range(3):
-        TS(V("Q3", 128 * l, 128 * l + 128), M("XQ"), float(l), A_.is_equal)
-    TS(M("NI"), M("IDN"), -1.0, A_.mult)
-    for i in range(16):
-        TS(L(i), M("CMT"), float(i + 1), A_.is_equal, 8.0, A_.mult)
-    TS(M("GP"), M("G1"), PF(2), A_.mult)
+
+    def spread_rows(l):
+        for r in (2 * l, 2 * l + 1, 6 + 2 * l, 7 + 2 * l):
+            TS(V("SR1", 128 * r, 128 * r + 128), M("XE"), float(r), A_.is_equal)
+            TS(V("SR2", 128 * r, 128 * r + 128), M("XO"), float(r), A_.is_equal)
 
     p96 = (0, 96)
-    CP(V("F1", 0, 256, 1, p96), V("KR", 0, 256, 1, p96))
-    TT(V("F2", 0, 256, 1, p96), V("KR", 0, 256, 1, p96), V("F1", 0, 256, 1, p96), A_.subtract)
-    for l in range(3):
+
+    def spread_kids(l):
         for side in range(2):
-            bank = "B%d" % (2 * l + side)
+            bank = "B%d" % (2 * (l % 2) + side)
             for half in range(2):
                 r = 6 * side + 2 * l + half
                 MM(V(bank, 256 * half, 256 * half + 256),
                    [(V("SR1", 128 * r, 128 * r + 128, 1, p96), V("F1", 0, 256, 1, p96)),
                     (V("SR2", 128 * r, 128 * r + 128, 1, p96), V("F2", 0, 256, 1, p96))])
             c = 1024 * l + 512 * side
-            if side == 0:
-                ACT(V("K", c, c + 512), V(bank, 0, 512))
-            else:
-                CP(V("K", c, c + 512), V(bank, 0, 512))
-        if l == 0:
-            CP(V("MRB", 0, 512, 1, (0, 24)), V("MR", 0, 512, 1, (0, 24)))
-        diag(V("B6", 64 * l, 64 * l + 64), "K", 1024 * l, 1024 * l + 1024)
-        TS(V("KWU", 64 * l, 64 * l + 64), V("B6", 64 * l, 64 * l + 64), 1.0 / 64, A_.mult)
+            ACT(V("K", c, c + 512), V(bank, 0, 512))
+
+    def types(l):
         MM(V("B7", 0, 512), [(V("Q3", 128 * l, 128 * l + 128, 1, (0, 24)), V("MRB", 0, 512, 1, (0, 24)))])
-        TS(V("SGN", SOFF[l], SOFF[l] + 512), V("B7", 0, 512), 2.0, A_.mult, -1.0, A_.add)
-        if l == 2:
-            TS(V("SC0", 0, 512), V("B7", 0, 512), 255.0, A_.mult, 1.0, A_.add)
 
-    KAB, CAB = w(64), w(64)
-    KD, CD = w(), w()
-    JW = V("JW", 0, 32)
-    NN, G5 = w(64), w(64)
-
-    def top_tables(bank, a):
-        TS(KAB, V(bank, a, a + 64), 1.0 / 64, A_.mult)
-        TS(NN, KAB, float(-NODE0), A_.add, 0.0, A_.max)
-        TS(G5, NN, 512.0, A_.is_ge, 512.0, A_.mult)
-        TT(KD, sub(KAB, 32, 64), sub(KAB, 0, 32), A_.subtract)
-        TT(CAB, NN, G5, A_.add)
-        TT(CD, sub(CAB, 32, 64), sub(CAB, 0, 32), A_.subtract)
-
-    def level(l):
-        hi = NODE0 + 512 * l
-        for h in range(2):
-            c = 64 * l + 16 * h
-            ACT(V("GA", 256 * h, 256 * h + 256), IND(V("Y", 0, hi), V("KWU", c, c + 16)))
-            TT(V("NB", 256 * h, 256 * h + 256), IND(V("Y", 0, hi), V("KWU", c + 32, c + 48)),
-               V("SGN", SOFF[l] + 256 * h, SOFF[l] + 256 * h + 256), A_.mult)
-        for h in range(2):
-            s = (256 * h, 256 * h + 256)
-            TS(V("RB", *s), V("NB", *s), 0.0, A_.min)
-            MM(V("B%d" % h, 0, 256), [(M("IDN"), V("GA", *s)), (M("NI"), V("RB", *s))])
-        for h in range(2):
-            s = (256 * h, 256 * h + 256)
-            TT(V("VV", *s), V("B%d" % h, 0, 256), V("NB", *s), A_.max)
-        for h in range(2):
-            s = (256 * h, 256 * h + 256)
-            TS(V("Y", hi + s[0], hi + s[1]), V("VV", *s), 255.0, A_.min)
-
-    def kid_errors(D, tp, win, a0):
-        f = (0, 512)
-        TS(V("RB", *f), V("NB", *f), 0.0, A_.max)
-        MM(V("B0", *f), tp + [(M("IDN"), V("NB", *f)), (M("N256"), V("RB", *f))])
-        TT(V("XM", *f), V("B4", *f), V("GA", *f), A_.mult)
-        MM(V("B1", *f), tp + [(M("NI"), V("GA", *f)), (M("N254"), V("XM", *f))])
-        wa, wb = V(win, a0, a0 + 512), V(win, a0 + 512, a0 + 1024)
-        TT(V("TMA", *f), V("B0", *f), D, A_.min)
-        TS(wa, V("TMA", *f), 0.0, A_.max)
-        MM(V("B2", *f), [(M("NI"), V("GA", *f)), (M("IDN"), wa)])
-        TT(V("TMB", *f), V("B1", *f), D, A_.min)
-        ACT(V("AB", 0, 512), V("B2", *f), F_.Abs)
-        TS(wb, V("TMB", *f), 0.0, A_.max)
-        MM(V("B3", *f), [(M("N2"), V("RB", *f)), (M("IDN"), V("NB", *f)), (M("IDN"), wb)])
-        ACT(V("AB", 512, 1024), V("B3", *f), F_.Abs)
-        diag(V("B5", 0, 64), "AB", 0, 1024)
-
-    level(0)
-    for nm, c in (("HI", 0.5), ("N256", -256.0), ("N254", -254.0), ("N2", -2.0), ("I255", 255.0)):
+    spread_rows(0)
+    TT(M("CMT"), M("G1"), M("CM1"), A_.mult)
+    CP(V("F1", 0, 256, 1, p96), V("KR", 0, 256, 1, p96))
+    TT(V("F2", 0, 256, 1, p96), V("KR", 0, 256, 1, p96), V("F1", 0, 256, 1, p96), A_.subtract)
+    spread_kids(0)
+    for l in range(3):
+        TS(V("Q3", 128 * l, 128 * l + 128), M("XQ"), float(l), A_.is_equal)
+    CP(V("MRB", 0, 512, 1, (0, 24)), V("MR", 0, 512, 1, (0, 24)))
+    types(0)
+    ACT(V("SGN", SOFF[0], SOFF[0] + 512), V("B7", *f), F_.Copy, -1.0, 2.0)
+    for i in range(16):
+        TS(L(i), M("CMT"), float(i + 1), A_.is_equal, 8.0, A_.mult)
+    spread_rows(1)
+    for nm, c in (("NI", -1.0), ("I128", 128.0), ("N256", -256.0), ("N254", -254.0), ("N2", -2.0), ("I255", 255.0)):
         TS(M(nm), M("IDN"), c, A_.mult)
+    kid_lists(0, "B6")
+
+    def more0():
+        spread_kids(1)
+        types(1)
+        ACT(V("SGN", SOFF[1], SOFF[1] + 512), V("B7", *f), F_.Copy, -1.0, 2.0)
+        kid_lists(1, "B6")
+        spread_rows(2)
+
+    TS(M("GP"), M("G1"), PF(2), A_.mult)
+    level(0, more0)
+    spread_kids(2)
     for i in range(16):
         SEL(V("LP", 128 * i, 128 * i + 128), M("GP"), [[0, 8], [1, 16]], -i, 0)
-    IOTA(JW, [[16, 32]], 0, 0)
-    IOTA(V("KC", 0, 4), [[16, 4]], 0, 0)
-    IOTA(V("DM", 0, 64), [[0, 4], [1, 16]], 0, 0)
-    IOTA(V("K1R", 0, 64), [[1, 64]], 1, 0)
-    IOTA(V("KR0", 0, 64), [[1, 64]], 0, 0)
-    IOTA(M("KT"), [[16, 4], [0, 32]], 0, 0)
-    IOTA(V("MT", 0, 256), [[1, 8], [0, 32]], 0, 0)
-    TT(V("T1", 0, 512), V("D0", 0, 512), V("SC0", 0, 512), A_.mult)
-    level(1)
-    top_tables("B6", 128)
-    TS(M("NG"), M("G1"), -1.0, A_.mult)
-    CP(M("G1F"), M("G1"))
-    TS(M("GL"), M("CM1"), PF(2), A_.is_gt)
-    TT(M("GL"), M("GL"), M("G1"), A_.mult)
-    TS(JW, JW, PF(2), A_.add)
-    TS(V("KC", 0, 4), V("KC", 0, 4), PF(2), A_.add)
-    TS(V("KJ", 0, 4), V("KC", 0, 4), 3072.0, A_.add)
-    TS(V("DM", 0, 64), V("DM", 0, 64), PF(2), A_.is_equal)
-    TS(M("KT"), M("KT"), PF(2), A_.add)
-    TS(PF(4), PF(2), 0.0, A_.is_equal)
-    TS(V("KR0", 0, 64), V("KR0", 0, 64), PF(4), A_.mult)
-    CP(V("CW", 0, 2), V("WTI", 0, 2))
-    FILL(V("YC", 512, 528), -1.0)
-    FILL(V("PM", 0, 48), -1.0)
-    FILL(V("KEYW", 0, 48), 0.0)
-    FILL(V("DONW", 0, 48), 0.0)
-    TS(V("KOL", 0, 8), V("G1", 0, 128, 16), 0.125, A_.mult)
 
-    base = wtop[0]
+    def more1():
+        types(2)
+        ACT(V("SGN", SOFF[2], SOFF[2] + 512), V("B7", *f), F_.Copy, -1.0, 2.0)
+        kid_lists(2, "B6")
+        TT(V("MD0", *f), V("B7", *f), V("D0", *f), A_.mult)
+        top_tables("B6")
+        grandkids(0)
+
+    level(1, more1)
+    grandkids(1)
+    diag(V("B7", 0, 64), "FFA", 0, 1024)
+    TS(sub(GKF, 0, 64), V("B7", 0, 64), 1.0 / 64, A_.mult)
+
+    def constants1():
+        TS(M("NG"), M("G1"), -1.0, A_.mult)
+        CP(M("G1F"), M("G1"))
+        TS(M("GL"), M("CM1"), PF(2), A_.is_gt)
+        TS(JW, JW, PF(2), A_.add)
+        TS(V("KC", 0, 4), V("KC", 0, 4), PF(2), A_.add)
+        TS(V("DM", 0, 64), V("DM", 0, 64), PF(2), A_.is_equal)
+        TS(M("KT"), M("KT"), PF(2), A_.add)
+        TS(PF(4), PF(2), 0.0, A_.is_equal)
+
+    def constants2():
+        TT(M("GL"), M("GL"), M("G1"), A_.mult)
+        TS(V("CW", 0, 2), V("WTI", 0, 2), 0.125, A_.mult)
+        FILL(V("YC", 512, 528), -1.0)
+        FILL(V("PM", 0, 48), -1.0)
+        FILL(V("KEYW", 0, 48), 0.0)
+        FILL(V("DONW", 0, 48), 0.0)
+        TS(V("KJ", 0, 4), V("KC", 0, 4), 3072.0, A_.add)
+        TS(V("KC2", 0, 4), V("KC", 0, 4), 129.0 / 128, A_.mult, 3072.0, A_.add)
+        TS(V("KR0", 0, 64), V("KR0", 0, 64), PF(4), A_.mult)
+        TS(V("KOL", 0, 8), V("G1", 0, 128, 16), 0.125, A_.mult)
+
     CC = w(4)
-    EW, TB1, EM1, T5, DL, M1, COL, C1, LIVE, LV5, P5 = w(64), w(), w(), w(), w(), w(), w(), w(), w(), w(), w()
-    K2F, EW2, TB2, EM2, X1, X2, X3, DL2, E8, KY1, KY2 = w(64), w(64), w(), w(), w(), w(), w(), w(), w(), w(), w()
-    US, S1, S2, S4, CD8, RUN, BEST = w(64), w(), w(64), w(128), w(256), w(64), w()
-    SW, BI1, BI2, A1, A2, O1, O2, O3, VA = w(4), w(4), w(4), w(4), w(4), w(4), w(4), w(4), w(4)
+    EA1, TB1, EM1, T5, DL, M1, COL, C1, LIVE, LV5, P5 = w(), w(), w(), w(), w(), w(), w(), w(), w(), w(), w()
+    K2F, K2X, EA2, TB2, EM2, X1, X2, X3, DL2, E8, KY1, KY2 = w(64), w(64), w(), w(), w(), w(), w(), w(), w(), w(), w(), w()
+    US, S1, S2, S4, CD8, RUN, BEST = w(), w(), w(64), w(128), w(256), w(64), w()
+    SW, BI2, A1, A2, O1, O3, VA = w(4), w(4), w(4), w(4), w(4), w(4), w(4)
     I0, I1, I2, I3, I4, I5 = [V("WI", 32 * k, 32 * k + 32) for k in range(6)]
-    f = (0, 512)
+    SG0 = V("SGN", SOFF[2], SOFF[2] + 512)
+    LW = V("LIBW", 0, 3840)
 
     for t in range(3):
-        MM(V("B4", *f), [(M("HI"), V("SGN", SOFF[2], SOFF[2] + 512)), (M("HI"), V("ONE", *f))])
         ACT(V("GA", *f), IND(V("Y", 0, 3328), V("KWU", 128, 160)))
-        TT(V("NB", *f), IND(V("Y", 0, 3328), V("KWU", 160, 192)), V("SGN", SOFF[2], SOFF[2] + 512), A_.mult)
-        kid_errors(V("D0", *f), [(M("IDN"), V("T1", *f))], "WIN", 0)
-        CP(EW, V("B5", 0, 64))
-        TT(TB1, sub(EW, 32, 64), sub(EW, 0, 32), A_.is_lt)
+        TT(V("NB", *f), IND(V("Y", 0, 3328), V("KWU", 160, 192)), SG0, A_.mult)
+
+        def tail():
+            if t == 0:
+                grandkids(2)
+            grandkids(3)
+            TT(KD, sub(KAB, 32, 64), sub(KAB, 0, 32), A_.subtract)
+            TT(CD, sub(CAB, 32, 64), sub(CAB, 0, 32), A_.subtract)
+            if t == 0:
+                constants2()
+            else:
+                a = 64 * (t - 1)
+                CP(V("LIBW", a, a + 64), V("Y", a, a + 64))
+                CP(V("LIBW", LIB + a, LIB + a + 64), V("Y", a, a + 64))
+
+        kid_errors(V("D0", *f), V("MD0", *f), SG0, "WIN", 0, EA1, SCHED1, constants1 if t == 0 else None, tail)
+        diag(V("B7", 64, 128), "FFB", 0, 1024)
+        TT(TB1, V("B6", 0, 32), EA1, A_.is_lt)
         TT(M1, TB1, CD, A_.mult)
-        TT(COL, M1, sub(CAB, 0, 32), A_.add)
-        CP(V("LU", 0, 32), COL)
-        CP(V("FF", 0, 512), IND(V("K", 0, 1536), V("LU", 0, 32)))
-        ACT(V("FF", 512, 1024), IND(V("K", 512, 2048), V("LU", 0, 32)))
-        ACT(V("SG2", *f), IND(V("SGN", 0, 1536), V("LU", 0, 32)))
-        diag(V("B6", 0, 64), "FF", 0, 1024)
-        MM(V("B4", *f), [(M("HI"), V("ONE", *f)), (M("HI"), V("SG2", *f))])
         TS(T5, TB1, 512.0, A_.mult)
+        TT(COL, M1, sub(CAB, 0, 32), A_.add)
         TT(DL, T5, JW, A_.add)
+        CP(V("LU", 0, 32), COL)
+        ACT(V("SG2", *f), IND(V("SGN", 0, 1536), V("LU", 0, 32)))
         CP(V("DLU", 0, 32), DL)
-        ACT(V("WIN2", *f), IND(V("WIN", 0, 1024), V("DLU", 0, 32)))
+        TS(sub(GKF, 64, 128), V("B7", 64, 128), 1.0 / 64, A_.mult)
+        TT(GKD, sub(GKF, 64, 128), sub(GKF, 0, 64), A_.subtract)
+        TT(sub(K2X, 0, 32), TB1, sub(GKD, 0, 32), A_.mult)
+        TT(sub(K2X, 32, 64), TB1, sub(GKD, 32, 64), A_.mult)
+        TT(EM1, V("B6", 0, 32), EA1, A_.min)
+        TT(K2F, K2X, sub(GKF, 0, 64), A_.add)
         TT(M1, TB1, KD, A_.mult)
-        TT(C1, M1, sub(KAB, 0, 32), A_.add)
-        TS(V("K2U", 0, 64), V("B6", 0, 64), 1.0 / 64, A_.mult)
+        CP(V("K2U", 0, 64), K2F)
+        CP(V("WIN2", *f), IND(V("WIN", 0, 1024), V("DLU", 0, 32)))
         ACT(V("GA", *f), IND(V("Y", 0, 2816), V("K2U", 0, 32)))
         TT(V("NB", *f), IND(V("Y", 0, 2816), V("K2U", 32, 64)), V("SG2", *f), A_.mult)
-        TT(V("MD", *f), V("B4", *f), V("WIN2", *f), A_.mult)
-        TT(EM1, sub(EW, 32, 64), sub(EW, 0, 32), A_.min)
-        TS(LIVE, C1, float(NODE0), A_.is_ge)
-        TS(K2F, V("B6", 0, 64), 1.0 / 64, A_.mult)
-        TS(LV5, LIVE, 512.0, A_.mult)
-        TT(P5, LV5, JW, A_.add)
-        kid_errors(V("WIN2", *f), [(M("IDN"), V("WIN2", *f)), (M("I255"), V("MD", *f))], "WIN2", 512)
-        TT(KD if t > 5 else X3, sub(K2F, 32, 64), sub(K2F, 0, 32), A_.subtract)
-        CP(EW2, V("B5", 0, 64))
-        TT(TB2, sub(EW2, 32, 64), sub(EW2, 0, 32), A_.is_lt)
+        TT(C1, M1, sub(KAB, 0, 32), A_.add)
+
+        def tail2():
+            TS(LIVE, C1, float(NODE0), A_.is_ge)
+            TT(X3, sub(K2F, 32, 64), sub(K2F, 0, 32), A_.subtract)
+            TS(LV5, LIVE, 512.0, A_.mult)
+            TS(KY1, DL, 2048.0, A_.add)
+            TT(P5, LV5, JW, A_.add)
+
+        kid_errors(V("WIN2", *f), V("MD", *f), V("SG2", *f), "WIN2", 512, EA2, SCHED2, None, tail2)
+        TT(TB2, V("B6", 0, 32), EA2, A_.is_lt)
+        TT(EM2, V("B6", 0, 32), EA2, A_.min)
         TT(X1, TB2, LV5, A_.mult)
-        TT(DL2, X1, P5, A_.add)
-        CP(V("LU", 32, 64), DL2)
-        ACT(V("DC", 0, 512), IND(V("WIN2", 0, 1536), V("LU", 32, 64)), F_.Copy, None, V("CW", 0, 1))
-        CP(V("DN", *f), IND(V("WIN2", 0, 1536), V("LU", 32, 64)))
-        TS(V("DC", 512, 1024), V("DN", *f), V("CW", 1, 2), A_.mult)
-        diag(V("B7", 0, 64), "DC", 0, 1024)
-        TT(EM2, sub(EW2, 32, 64), sub(EW2, 0, 32), A_.min)
         TT(X3, X3, TB2, A_.mult)
+        TT(DL2, X1, P5, A_.add)
         TT(EM2, EM2, EM1, A_.subtract)
+        CP(V("LU", 32, 64), DL2)
+        W2 = IND(V("WIN2", 0, 1536), V("LU", 32, 64))
+        ACT(V("DC", 0, 512), W2, F_.Copy, None, V("CW", 0, 1))
+        TS(V("DC", 512, 1024), W2, V("CW", 1, 2), A_.mult)
+        ACT(V("DN", *f), W2)
+        diag(V("B7", 0, 64), "DC", 0, 1024)
         TT(X3, X3, sub(K2F, 0, 32), A_.add)
         TT(EM2, EM2, LIVE, A_.mult)
         TT(X3, X3, C1, A_.subtract)
         TT(E8, EM2, EM1, A_.add)
         TT(X3, X3, LIVE, A_.mult)
-        TS(US, V("B7", 0, 64), 0.125, A_.mult)
-        U1, U2 = sub(US, 0, 32), sub(US, 32, 64)
-        TT(I0, U1, U2, A_.mult)
-        CP(I3, U1)
-        TS(I1, I0, 5, A_.arith_shift_right)
+        TS(KY2, TB2, 512.0, A_.mult)
+        TT(X3, X3, C1, A_.add)
+        TS(US, V("B7", 0, 32), 32.0, A_.add)
+        TS(I3, V("B7", 0, 32), 0.0, A_.add)
+        TT(I0, V("B7", 32, 64), US, A_.mult)
         TS(I4, I3, 127, A_.bitwise_and)
-        TT(I2, I1, U2, A_.add)
+        TS(I5, I0, 5, A_.arith_shift_right, 2047, A_.bitwise_and)
         TS(S1, I4, 2.0, A_.mult, 1.0, A_.add)
-        TS(I5, I2, 2047, A_.bitwise_and)
-        TS(sub(S2, 0, 32), I4, 4.0, A_.mult, 2.0, A_.add)
         CP(V("CU", 0, 32), I5)
-        ACT(V("CG", 0, 512), IND(V("LIBW", 0, 3840), V("CU", 0, 32)))
+        ACT(V("CG", 0, 512), IND(LW, V("CU", 0, 32)))
         CP(sub(CD8, 0, 32), I5)
+        TS(sub(S2, 0, 32), I4, 4.0, A_.mult, 2.0, A_.add)
         TS(sub(S2, 32, 64), I4, 4.0, A_.mult, 2.0, A_.add)
         TT(sub(CD8, 32, 64), sub(CD8, 0, 32), S1, A_.add)
-        CP(V("CU", 32, 64), sub(CD8, 32, 64))
-        ACT(V("CG", 512, 1024), IND(V("LIBW", 0, 3840), V("CU", 32, 64)))
+        CP(V("CHU", 0, 32), X3)
         TT(sub(CD8, 64, 128), sub(CD8, 0, 64), S2, A_.add)
+        CP(V("CU", 32, 64), sub(CD8, 32, 64))
         CP(V("CU", 64, 128), sub(CD8, 64, 128))
+        ACT(V("CG", 512, 1024), IND(LW, V("CU", 32, 64)))
+
+        def cand(m, buf):
+            TT(V(buf, 512 * (m % 2), 512 * (m % 2) + 512), IND(LW, V("CU", 32 * m, 32 * m + 32)), V("DN", *f), A_.subtract)
+
+        cand(2, "XA0")
         for h in range(2):
-            s = (512 * h, 512 * h + 512)
-            TT(V("XA0", *s), IND(V("LIBW", 0, 3840), V("CU", 64 + 32 * h, 96 + 32 * h)), V("DN", *f), A_.subtract)
-            MM(V("B%d" % (2 + h), *f), [(M("NI"), V("DN", *f)), (M("IDN"), V("CG", *s))])
-        for h in range(2):
+            MM(V("B%d" % (2 + h), *f), [(M("NI"), V("DN", *f)), (M("IDN"), V("CG", 512 * h, 512 * h + 512))])
             ACT(V("AC0", 512 * h, 512 * h + 512), V("B%d" % (2 + h), *f), F_.Abs)
         diag(V("B5", 0, 64), "AC0", 0, 1024, [(M("IDN"), V("MT", 0, 64))])
-        for h in range(2):
-            TS(sub(S4, 64 * h, 64 * h + 64), S2, 2.0, A_.mult)
-        TT(sub(CD8, 128, 256), sub(CD8, 0, 128), S4, A_.add)
-        CP(V("CU", 128, 256), sub(CD8, 128, 256))
+        TS(sub(S4, 0, 64), S2, 2.0, A_.mult)
+        TS(sub(S4, 64, 128), S2, 2.0, A_.mult)
+        cand(3, "XA0")
         ACT(V("AC1", 0, 1024), V("XA0", 0, 1024), F_.Abs)
         diag(V("B6", 0, 64), "AC1", 0, 1024, [(M("IDN"), V("MT", 64, 128))])
-        for h in range(2):
-            TT(V("XA1", 512 * h, 512 * h + 512), IND(V("LIBW", 0, 3840), V("CU", 128 + 32 * h, 160 + 32 * h)), V("DN", *f), A_.subtract)
-        ACT(V("AC0", 0, 1024), V("XA1", 0, 1024), F_.Abs)
-        TT(X3, X3, C1, A_.add)
-        CP(V("CHU", 0, 32), X3)
+        TT(sub(CD8, 128, 256), sub(CD8, 0, 128), S4, A_.add)
+        CP(V("CU", 128, 256), sub(CD8, 128, 256))
+        cand(4, "XA1")
         CP(RUN, V("B5", 0, 64))
-        diag(V("B5", 0, 64), "AC0", 0, 1024, [(M("IDN"), V("MT", 128, 192))])
-        for h in range(2):
-            s = (512 * h, 512 * h + 512)
-            TT(V("XA2", *s), IND(V("LIBW", 0, 3840), V("CU", 192 + 32 * h, 224 + 32 * h)), V("DN", *f), A_.subtract)
-            ACT(V("AC1", *s), V("XA2", *s), F_.Abs)
-            if h == 0:
-                TT(RUN, V("B6", 0, 64), RUN, A_.min)
-        diag(V("B6", 0, 64), "AC1", 0, 1024, [(M("IDN"), V("MT", 192, 256))])
-        ACT(V("YC", *f), IND(V("Y", 0, 3840), V("CHU", 0, 32)))
-        TT(RUN, V("B5", 0, 64), RUN, A_.min)
+        cand(5, "XA1")
+        ACT(V("AC2", 0, 1024), V("XA1", 0, 1024), F_.Abs)
+        diag(V("B5", 0, 64), "AC2", 0, 1024, [(M("IDN"), V("MT", 128, 192))])
+        cand(6, "XA2")
+        ACT(V("AC3", 0, 512), V("XA2", 0, 512), F_.Abs)
+        diag(V("B7", 0, 32), "AC3", 0, 512, [(M("IDN"), V("MT", 192, 224))])
         TT(RUN, V("B6", 0, 64), RUN, A_.min)
-        TT(BEST, sub(RUN, 0, 32), sub(RUN, 32, 64), A_.min)
+        cand(7, "XA2")
+        ACT(V("AC3", 512, 1024), V("XA2", 512, 1024), F_.Abs)
+        diag(V("B6", 0, 32), "AC3", 512, 1024, [(M("IDN"), V("MT", 224, 256))])
+        ACT(V("YC", *f), IND(V("Y", 0, 3840), V("CHU", 0, 32)) if t > 5 else IND(V("Y", 0, 3328), V("CHU", 0, 32)))
+        TT(RUN, V("B5", 0, 64), RUN, A_.min)
+        TT(KY2, KY2, COL, A_.add)
+        TT(sub(RUN, 0, 32), sub(RUN, 0, 32), sub(RUN, 32, 64), A_.min)
+        TT(KY2, KY2, KY1, A_.subtract)
+        TT(sub(RUN, 0, 32), V("B7", 0, 32), sub(RUN, 0, 32), A_.min)
+        TT(KY2, KY2, LIVE, A_.mult)
+        TT(KY2, KY2, KY1, A_.add)
+        TS(V("KEYW", 0, 32), KY2, 128.0, A_.mult)
+        TT(BEST, V("B6", 0, 32), sub(RUN, 0, 32), A_.min)
         TT(V("BB", 0, 32), BEST, E8, A_.is_lt)
+        CP(I0, BEST)
         op("v", [("ONE", 0, 32), ("BB", 0, 32)], [("INC", 0, 32)],
            lambda: g.vector.tensor_tensor_scan(T.INC[:, 0:32], T.ONE[:, 0:32], T.BB[:, 0:32], 0.0, A_.mult, A_.add))
+        TS(I1, I0, 7, A_.bitwise_and)
         for q in range(4):
             MM(V("B0", 32 * q, 32 * q + 32), [(M("G1"), V("INC", 0, 32))])
-        MM(V("B1", 0, 32), [(M("G1"), V("INC", 0, 32)), (M("NG"), V("BB", 0, 32)), (M("GL"), V("BB", 0, 32))])
+        MM(V("B1", 0, 32), [(M("NG"), V("BB", 0, 32)), (M("GL"), V("BB", 0, 32)), (M("G1"), V("INC", 0, 32))])
+        TT(X1, I1, S1, A_.mult)
         TT(M("CMP"), V("B0", 0, 128), M("KT"), A_.is_le)
         TT(V("PM", 0, 32), V("B1", 0, 32), V("BB", 0, 32), A_.mult)
         for q in range(4):
             RED(sub(CC, q, q + 1), V("CMP", 32 * q, 32 * q + 32))
+        TT(X1, X1, sub(CD8, 0, 32), A_.add)
         CP(V("CCU", 0, 4), CC)
         TS(V("CC16", 0, 4), CC, 16.0, A_.mult)
         TT(V("OH", 0, 64), IND(V("PM", 0, 48), V("CCU", 0, 4)), V("K1R", 0, 64), A_.is_equal)
         MM(V("B2", 0, 4), [(M("IDN"), V("CC16", 0, 4))] + [(V("LP", 128 * i, 128 * i + 128), V("OH", i, 64, 16)) for i in range(16)])
+        TS(X2, X1, 2048.0, A_.is_ge, 2048.0, A_.mult)
+        TT(V("DONW", 0, 32), X1, X2, A_.subtract)
+        TT(V("VK", 0, 64), IND(V("KEYW", 0, 48), V("CCU", 0, 4)), V("OH", 0, 64), A_.mult)
+        TS(VA, CC, 32.0, A_.is_lt)
         CP(V("JLU", 0, 4), V("B2", 0, 4))
         SND = "SND%d" % t
         CP(V(SND, 0, 64), IND(V("YC", 0, 528), V("JLU", 0, 4)))
         waits("g", [(SND, 0, 64)], [])
         land = "LAND%d" % t if hop is None else "RLY%d" % t
         g.remote_dma(T[land][:], T[SND][:], T.sem[("arr%d" if hop is None else "hop%d") % t], T.sem["snt%d" % t], spid, srid, smask)
-        TS(KY1, DL, 2048.0, A_.add)
-        TS(KY2, TB2, 512.0, A_.mult)
-        CP(I0, BEST)
-        TT(KY2, KY2, COL, A_.add)
-        TS(I1, I0, 7, A_.bitwise_and)
-        TT(KY2, KY2, KY1, A_.subtract)
-        TT(X1, I1, S1, A_.mult)
-        TT(KY2, KY2, LIVE, A_.mult)
-        TT(X1, X1, sub(CD8, 0, 32), A_.add)
-        TT(KY2, KY2, KY1, A_.add)
-        TS(X2, X1, 2048.0, A_.is_ge, 2048.0, A_.mult)
-        TS(V("KEYW", 0, 32), KY2, 128.0, A_.mult)
-        TT(V("DONW", 0, 32), X1, X2, A_.subtract)
-        TT(V("VK", 0, 64), IND(V("KEYW", 0, 48), V("CCU", 0, 4)), V("OH", 0, 64), A_.mult)
         TT(V("VD", 0, 64), IND(V("DONW", 0, 48), V("CCU", 0, 4)), V("OH", 0, 64), A_.mult)
-        MM(V("B3", 0, 64), [(M("G1F"), V("VK", 0, 64)), (M("G1F"), V("KR0", 0, 64))])
+        MM(V("B3", 0, 64), [(M("G1F"), V("KR0", 0, 64)), (M("G1F"), V("VK", 0, 64))])
         MM(V("B7", 0, 64), [(M("G1F"), V("VD", 0, 64))])
         TT(V("SWT", 0, 64), V("B3", 0, 64), V("DM", 0, 64), A_.mult)
+        CP(V("ROWS", 0, 64), V("B3", 0, 64))
         for q in range(4):
             RED(sub(SW, q, q + 1), V("SWT", 16 * q, 16 * q + 16))
-        TS(BI1, SW, -0.5, A_.add)
         TS(BI2, SW, -63.5, A_.add)
         for q in range(4):
-            ACT(V("SGJ", 0, 64), V("B3", 0, 64), F_.Sign, sub(BI1, q, q + 1), -1.0, sub(A1, q, q + 1))
-            ACT(V("SGJ", 0, 64), V("B3", 0, 64), F_.Sign, sub(BI2, q, q + 1), -1.0, sub(A2, q, q + 1))
+            TS(V("CMQ", 64 * q, 64 * q + 64), V("ROWS", 0, 64), sub(SW, q, q + 1), A_.is_lt)
+            ACT(V("SGJ", 0, 64), V("ROWS", 0, 64), F_.Sign, sub(BI2, q, q + 1), -1.0, sub(A2, q, q + 1))
+        for q in range(4):
+            RED(sub(A1, q, q + 1), V("CMQ", 64 * q, 64 * q + 64))
+        TS(O1, SW, 1.0 / 128, A_.mult)
         TS(V("TQ", 0, 64), V("B7", 0, 64), PF(3), A_.mult)
-        TS(VA, CC, 32.0, A_.is_lt)
-        TS(O1, SW, 1.0 / 128, A_.mult, -3072.0, A_.add)
+        TS(O3, A1, 2.0, A_.mult, -64.0, A_.add)
+        TT(O1, O1, V("KC2", 0, 4), A_.subtract)
         TT(V("SRC", 0, 64), V("B7", 0, 64), V("TQ", 0, 64), A_.subtract)
-        TS(O2, V("KC", 0, 4), 129.0 / 128, A_.mult)
-        TT(O1, O1, O2, A_.subtract)
         TT(O1, O1, VA, A_.mult)
-        TT(O3, A1, A2, A_.subtract)
-        TS(O3, O3, 1.0, A_.is_lt)
+        TT(O3, A2, O3, A_.is_equal)
         TT(O1, O1, O3, A_.mult)
         TT(O1, O1, V("KJ", 0, 4), A_.add)
         CP(V("OFU", 0, 4), O1)
         op("v", [("SRC", 0, 64), ("OFU", 0, 4)], [("K", 0, 3136)],
            lambda: g.vector.tensor_copy(out=T.K[:, 0:3136].indirect(T.OFU[:, 0:4]), in_=T.SRC[:, 0:64]))
-        for l in range(3):
-            diag(V("B4", 64 * l, 64 * l + 64), "K", 1024 * l, 1024 * l + 1024)
-        TS(V("KWU", 0, 192), V("B4", 0, 192), 1.0 / 64, A_.mult)
+        kid_lists(0, "B4")
+        kid_lists(2, "B6")
         if t < 2:
-            top_tables("B4", 128)
-        else:
-            for l in range(3):
-                for side in range(2):
-                    c = 1024 * l + 512 * side
-                    bank = "B%d" % (5 + side)
-                    p8 = (0, 8)
-                    MM(V(bank, 0, 512, 1, p8), [(V("KOL", 0, 8), V("K", c, c + 512))])
-                    o = 1536 * side + 512 * l
-                    ACT(V("KOB", o, o + 512, 1, p8), V(bank, 0, 512, 1, p8))
-            waits("s", [("KOB", 0, 3072)], [])
-            DMA("s", T.ko[:], T.KOB[0:8, :], [("KOB", 0, 3072)], [])
+            top_tables("B6")
+            grandkids(0)
+        kid_lists(1, "B5")
         a = 64 * t
         g.vector.wait_ge(T.sem["arr%d" % t], acnt)
         lnd = V("LAND%d" % t, 0, 64)
         TS(V("MGM", 0, 64), lnd, 0.0, A_.is_lt)
         TT(V("MGO", 0, 64), V("Y", a, a + 64), V("MGM", 0, 64), A_.mult)
         TT(V("Y", a, a + 64), lnd, V("MGO", 0, 64), A_.max)
-        if t == 2:
-            DMA("s", T.yo[:, 0:NODE0], T.Y[:, 0:NODE0], [("Y", 0, NODE0)], [])
-        level(0)
         if t < 2:
-            CP(V("LIBW", a, a + 64), V("Y", a, a + 64))
-            CP(V("LIBW", LIB + a, LIB + a + 64), V("Y", a, a + 64))
+            level(0, lambda: grandkids(1))
+            diag(V("B7", 0, 64), "FFA", 0, 1024)
+            level(1, lambda: grandkids(2))
+            TS(sub(GKF, 0, 64), V("B7", 0, 64), 1.0 / 64, A_.mult)
         else:
-            DMA("s", T.yo[:, NODE0:NODE0 + 512], T.Y[:, NODE0:NODE0 + 512], [("Y", NODE0, NODE0 + 512)], [])
-        level(1)
-        if t == 2:
-            DMA("s", T.yo[:, 2816:3328], T.Y[:, 2816:3328], [("Y", 2816, 3328)], [])
-            level(2)
-            DMA("s", T.yo[:, 3328:3840], T.Y[:, 3328:3840], [("Y", 3328, 3840)], [])
+            def kids_out(l):
+                for side in range(2):
+                    c, o, bank, p8 = 1024 * l + 512 * side, 1536 * side + 512 * l, "B%d" % (5 + side), (0, 8)
+                    MM(V(bank, 0, 512, 1, p8), [(V("KOL", 0, 8), V("K", c, c + 512))])
+                    ACT(V("KOB", o, o + 512, 1, p8), V(bank, 0, 512, 1, p8))
+            DMA("s", T.yo[:, 0:NODE0], T.Y[:, 0:NODE0], [("Y", 0, NODE0)], [])
+            for l in range(3):
+                level(l, lambda: kids_out(l))
+                if l == 2:
+                    DMA("s", T.ko[:], T.KOB[0:8, :], [("KOB", 0, 3072)], [])
+                h = NODE0 + 512 * l
+                DMA("s", T.yo[:, h:h + 512], T.Y[:, h:h + 512], [("Y", h, h + 512)], [])
 
     for t in range(3):
         g.wait_ge(T.sem["snt%d" % t], scnt)

from concourse.mybir import AluOpType, AxisListType, ActivationFunctionType

A_ = AluOpType
F_ = ActivationFunctionType

SCRATCH = {}
for _t, _s in (
        ("bfloat16", "Y 3840 LIBW 3840 K 3136 F1 256 F2 256 MRB 512 SGN 1536 D0 512 MD0 512 ONE 512 IDN 128 NI 128 I128 128 I255 128 N256 128 "
                     "N254 128 N2 128 CMG 128 CM1 128 G1 128 NG 128 GL 128 GP 128 CMT 128 L8 2048 LP 2048 X96 128 SR1 1536 PAR 128 XE 128 XO 128 "
                     "SR2 1536 XQ 128 Q3 384 KOL 8 KT 128 K1R 64 MT 256 GA 512 NB 512 RB 512 VV 512 XM 512 MD 512 TMA 512 TMB 512 WIN 1024 "
                     "WIN2 1536 AB 1024 FFA 1024 FFB 1024 SG2 512 DN 512 DC 1024 CG 1024 XA0 1024 XA1 1024 XA2 1024 AC0 1024 AC1 1024 AC2 1024 "
                     "AC3 1024 YC 528 BB 32 INC 32 CMP 128 CC16 4 OH 64 TQ 64 SRC 64 MGM 64 MGO 64"),
        ("float32", "CW 2 PF 8 G1F 128 KR0 64 DM 64 JW 32 KC 4 KJ 4 KC2 4 WR 2560 PM 48 KEYW 48 DONW 48 VK 64 VD 64 ROWS 64 SWT 64 SGJ 64 CMQ 256 KOB 3072"),
        ("int32", "KR 256 MR 512 WTI 2 PI 8 WI 256"),
        ("uint16", "KWU 192 CABU 64 LU 64 K2U 64 DLU 32 CHU 32 CU 256 CCU 4 JLU 4 OFU 4")):
    _w = _s.split()
    for _k in range(0, len(_w), 2):
        SCRATCH[_w[_k]] = ("sbuf", [128, int(_w[_k + 1])], _t)
for _k in range(3):
    for _n in ("SND", "LAND", "RLY"):
        SCRATCH["%s%d" % (_n, _k)] = ("sbuf", [128, 64], "bfloat16")
for _k in range(8):
    SCRATCH["B%d" % _k] = ("psum", [128, 512], "float32")

SEMAPHORES = ["qv", "qa", "qp", "qg"] + ["d%d" % k for k in range(20)] + ["%s%d" % (n, k) for n in ("hop", "arr", "snt", "rst") for k in range(3)]

LIB, NODE0 = 2048, 2304
SOFF = (0, 1024, 512)


def ring_relay(topo, core, dst):
    if topo.may_write(core, dst):
        return None
    ok = [h for h in topo.cores_of(core) if h != core and topo.may_write(h, dst)]
    near = [h for h in ok if topo.die(h) == topo.die(core)]
    return (near + ok)[0]


def bits(topo, src, dst, n):
    e = topo.engines(src, dst)[:n]
    return sum(1 << k for k in e), len(e)


def relay_program(g, core, T, topo):
    n = len(T.cores)
    for r in range(n):
        dst = T.cores[(r + 1) % n]
        if ring_relay(topo, T.cores[r], dst) != core:
            continue
        _, got = bits(topo, T.cores[r], core, 8)
        mask, cnt = bits(topo, core, dst, 8)
        rid, pid = topo.addr(dst, core)
        for t in range(3):
            g.wait_ge(T.sem["hop%d" % t], got)
            g.remote_dma(T["LAND%d" % t][:], T["RLY%d" % t][:], T.sem["arr%d" % t], T.sem["rst%d" % t], pid, rid, mask)
        for t in range(3):
            g.wait_ge(T.sem["rst%d" % t], cnt)


def rank_program(g, core, T, topo):
    rank = T.rank_of(core)
    if rank is None:
        relay_program(g, core, T, topo)
        return
    nr = len(T.cores)
    dst = T.cores[(rank + 1) % nr]
    prev = T.cores[(rank - 1) % nr]
    hop = ring_relay(topo, core, dst)
    first = dst if hop is None else hop
    smask, scnt = bits(topo, core, first, 8)
    srid, spid = topo.addr(first, core)
    last = ring_relay(topo, prev, core)
    _, acnt = bits(topo, prev if last is None else last, core, 8)

    eng = {"v": g.vector, "a": g.scalar, "p": g.tensor, "g": g, "s": g.sync}
    cnt = {"v": 0, "a": 0, "p": 0, "g": 0}
    clock = {"v": {}, "a": {}, "p": {}, "g": {}, "s": {}}
    acc = {}
    nd = [0]
    seq = [0]

    def waits(q, reads, writes):
        need = []
        for lst, wr in ((reads, False), (writes, True)):
            for nm, a, b in lst:
                ps = nm[0] == "B" and nm[1:].isdigit()
                for e in acc.get(nm, ()):
                    apart = e[1] <= a or e[0] >= b
                    if apart and (not ps or e[3] == q):
                        continue
                    if e[2] or wr or (ps and e[3] != q):
                        if e[3] == q and wr and (q == "p" or not e[2]):
                            continue
                        need.append((e[6], e[4], e[5], e[7]))
        need.sort(key=lambda x: -x[0])
        ck = clock[q]
        for _, sem, val, clk in need:
            if ck.get(sem, 0) >= val:
                continue
            eng[q].wait_ge(T.sem[sem], val)
            for k in clk:
                if ck.get(k, 0) < clk[k]:
                    ck[k] = clk[k]
            ck[sem] = max(val, ck.get(sem, 0))

    def note(q, clk, reads, writes, sem, val):
        clk = dict(clk)
        clk[sem] = val
        seq[0] += 1
        for lst, wr in ((reads, False), (writes, True)):
            for nm, a, b in lst:
                old = acc.get(nm, [])
                if wr:
                    old = [e for e in old if not (a <= e[0] and e[1] <= b)]
                else:
                    old = [e for e in old if not (a <= e[0] and e[1] <= b and not e[2] and e[3] == q)]
                old.append((a, b, wr, q, sem, val, seq[0], clk))
                acc[nm] = old

    def op(q, reads, writes, f):
        waits(q, reads, writes)
        cnt[q] += 1
        f().then_inc(T.sem["q" + q], 1)
        note(q, clock[q], reads, writes, "q" + q, cnt[q])

    def V(nm, a, b, st=1, p=None):
        if p is None:
            ap = T[nm][:, a:b] if st == 1 else T[nm][:, a:b:st]
        else:
            ap = T[nm][p[0]:p[1], a:b]
        return (ap, [(nm, a, b)])

    def IND(win, off):
        return (win[0].indirect(off[0]), win[1] + off[1])

    def TT(o, x, y, f):
        op("v", x[1] + y[1], o[1], lambda: g.vector.tensor_tensor(out=o[0], in0=x[0], in1=y[0], op=f))

    def TS(o, x, s1, f1, s2=None, f2=None):
        rd = list(x[1])
        a1 = s1
        if isinstance(s1, tuple):
            rd += s1[1]
            a1 = s1[0]
        if f2 is None:
            op("v", rd, o[1], lambda: g.vector.tensor_scalar(out=o[0], in0=x[0], scalar1=a1, scalar2=None, op0=f1))
        else:
            op("v", rd, o[1], lambda: g.vector.tensor_scalar(out=o[0], in0=x[0], scalar1=a1, scalar2=s2, op0=f1, op1=f2))

    def CP(o, x):
        op("v", x[1], o[1], lambda: g.vector.tensor_copy(out=o[0], in_=x[0]))

    def RED(o, x):
        op("v", x[1], o[1], lambda: g.vector.tensor_reduce(out=o[0], in_=x[0], axis=AxisListType.X, op=A_.add))

    def FILL(o, c):
        op("v", [], o[1], lambda: g.vector.memset(o[0], c))

    def ACT(o, x, f=F_.Copy, bias=None, scale=None, accum=None):
        rd, wr, kw = list(x[1]), list(o[1]), {}
        for nm, c in (("bias", bias), ("scale", scale)):
            if isinstance(c, tuple):
                rd += c[1]
                kw[nm] = c[0]
            elif c is not None:
                kw[nm] = c
        if accum is not None:
            wr += accum[1]
            kw["accum_out"] = accum[0]
        op("a", rd, wr, lambda: g.scalar.activation(out=o[0], in_=x[0], func=f, **kw))

    def mm(o, l, r, start, stop):
        op("p", l[1] + r[1], o[1], lambda: g.tensor.matmul(o[0], l[0], r[0], start, stop))

    def MM(o, prs):
        n = len(prs)
        for k in range(n):
            mm(o, prs[k][0], prs[k][1], k == 0, k == n - 1)

    def IOTA(o, pat, base, ch):
        op("g", [], o[1], lambda: g.iota(o[0], pat, base, ch, allow_small_or_imprecise_dtypes=True))

    def SEL(o, x, pat, base, ch):
        op("g", x[1], o[1], lambda: g.affine_select(o[0], x[0], pat, A_.is_equal, 0.0, base, ch))

    def DMA(q, o, x, reads, writes):
        sem = "d%d" % nd[0]
        nd[0] += 1
        waits(q, reads, writes)
        eng[q].dma_start(out=o, in_=x).then_inc(T.sem[sem], 16)
        note("dma" + sem, {}, reads, writes, sem, 16)

    def M(nm):
        return V(nm, 0, 128)

    wtop = [0]

    def w(n=32):
        a = wtop[0]
        wtop[0] += n
        return V("WR", a, a + n)

    def sub(x, a, b):
        nm, lo, _ = x[1][0]
        return V(nm, lo + a, lo + b)

    def L(i):
        return V("L8", 128 * i, 128 * i + 128)

    def diag(out, nm, lo, hi, more=()):
        MM(out, list(more) + [(L(i), V(nm, lo + i, hi, 16)) for i in range(16)])

    f = (0, 512)
    PI = lambda k: V("PI", k, k + 1)
    PF = lambda k: V("PF", k, k + 1)
    JW = V("JW", 0, 32)
    KAB, CAB, NN, G5, KD, CD = w(64), w(64), w(64), w(64), w(), w()
    GKF, GKD = w(128), w(64)

    def kid_lists(l, bank):
        diag(V(bank, 64 * l, 64 * l + 64), "K", 1024 * l, 1024 * l + 1024)
        TS(V("KWU", 64 * l, 64 * l + 64), V(bank, 64 * l, 64 * l + 64), 1.0 / 64, A_.mult)

    def top_tables(bank):
        TS(KAB, V(bank, 128, 192), 1.0 / 64, A_.mult)
        TS(NN, KAB, float(-NODE0), A_.add, 0.0, A_.max)
        TS(G5, NN, 512.0, A_.is_ge, 512.0, A_.mult)
        TT(CAB, NN, G5, A_.add)
        CP(V("CABU", 0, 64), CAB)

    def grandkids(k):
        off = V("CABU", 32 * (k // 2), 32 * (k // 2) + 32)
        o = V("FFA" if k < 2 else "FFB", 512 * (k % 2), 512 * (k % 2) + 512)
        win = V("K", 512 * (k % 2), 1536 + 512 * (k % 2))
        if k < 3:
            ACT(o, IND(win, off))
        else:
            CP(o, IND(win, off))

    def level(l, mid=None):
        hi = NODE0 + 512 * l
        hs = [(256 * h, 256 * h + 256) for h in range(2)]
        for h in range(2):
            c = 64 * l + 16 * h
            ACT(V("GA", *hs[h]), IND(V("Y", 0, hi), V("KWU", c, c + 16)))
            TT(V("NB", *hs[h]), IND(V("Y", 0, hi), V("KWU", c + 32, c + 48)), V("SGN", SOFF[l] + 256 * h, SOFF[l] + 256 * h + 256), A_.mult)
        if mid is not None:
            mid()
        for h in range(2):
            TS(V("RB", *hs[h]), V("NB", *hs[h]), 0.0, A_.min)
            MM(V("B%d" % h, 0, 256), [(M("IDN"), V("GA", *hs[h])), (M("NI"), V("RB", *hs[h]))])
        for h in range(2):
            TT(V("VV", *hs[h]), V("B%d" % h, 0, 256), V("NB", *hs[h]), A_.max)
        for h in range(2):
            TS(V("Y", hi + hs[h][0], hi + hs[h][1]), V("VV", *hs[h]), 255.0, A_.min)

    SCHED1 = ((0, "IDN", "D"), (0, "I255", "MDb"), (1, "IDN", "D"), (1, "I255", "MDb"), (4, "I128", "SG"), (4, "IDN", "GA"),
              (0, "IDN", "NB"), (0, "N256", "RB"), (1, "NI", "GA"), (1, "N254", "XM"))
    SCHED2 = ((7, "I128", "SG"), (4, "I128", "SG"), (7, "IDN", "D"), (0, "IDN", "D"), (1, "IDN", "D"), (4, "IDN", "GA"), (1, "NI", "GA"),
              (0, "IDN", "NB"), (0, "I255", "MDb"), (0, "N256", "RB"), (1, "I255", "MDb"), (1, "N254", "XM"))

    def kid_errors(D, MDb, SG, win, a0, EWA, sched, pre=None, mid=None):
        src = {"D": D, "MDb": MDb, "SG": SG}
        left = [e[0] for e in sched]
        seen = []
        for o, l, r in sched:
            if r == "MDb" and o == 0 and 7 in seen:
                ACT(MDb, V("B7", *f), F_.Relu, -128.0)
            if r == "RB":
                TS(V("RB", *f), V("NB", *f), 0.0, A_.max)
            if r == "XM":
                ACT(V("XM", *f), V("B4", *f), F_.Relu, -128.0)
            left.remove(o)
            mm(V("B%d" % o, *f), M(l), src[r] if r in src else V(r, *f), o not in seen, o not in left)
            seen.append(o)
        if pre is not None:
            pre()
        wa, wb = V(win, a0, a0 + 512), V(win, a0 + 512, a0 + 1024)
        TT(V("TMA", *f), V("B0", *f), D, A_.min)
        TS(wa, V("TMA", *f), 0.0, A_.max)
        TT(V("TMB", *f), V("B1", *f), D, A_.min)
        MM(V("B2", *f), [(M("NI"), V("GA", *f)), (M("IDN"), wa)])
        ACT(V("AB", 0, 512), V("B2", *f), F_.Abs)
        TS(wb, V("TMB", *f), 0.0, A_.max)
        MM(V("B3", *f), [(M("N2"), V("RB", *f)), (M("IDN"), V("NB", *f)), (M("IDN"), wb)])
        diag(V("B5", 0, 32), "AB", 0, 512)
        ACT(V("AB", 512, 1024), V("B3", *f), F_.Abs)
        if mid is not None:
            mid()
        CP(EWA, V("B5", 0, 32))
        diag(V("B6", 0, 32), "AB", 512, 1024)

    DMA("s", T.KR[0:96, :], T.kid[:], [], [("KR", 0, 256)])
    DMA("a", T.MR[0:24, :], T.mx[:], [], [("MR", 0, 512)])
    DMA("s", T.Y[:, 0:NODE0], T.lv[:], [], [("Y", 0, NODE0)])
    DMA("a", T.D0[:], T.tg[:], [], [("D0", 0, 512)])
    DMA("a", T.WTI[:], T.wt[:], [], [("WTI", 0, 2)])
    DMA("s", T.LIBW[:, 0:LIB], T.lv[:, 0:LIB], [], [("LIBW", 0, LIB)])
    DMA("s", T.LIBW[:, LIB:3840], T.lv[:, 0:1792], [], [("LIBW", LIB, 3840)])

    FILL(V("ONE", 0, 512), 1.0)
    op("g", [], PI(0)[1], lambda: g.iota(PI(0)[0], [[0, 1]], 0, 1))
    IOTA(M("PAR"), [[0, 64], [1, 2]], 0, 0)
    IOTA(M("X96"), [[-12, 8], [0, 16]], 0, 1)
    IOTA(M("CMG"), [[1, 8], [0, 16]], 0, 0)
    IOTA(M("CM1"), [[0, 8], [1, 16]], 1, 0)
    IOTA(M("XQ"), [[-3, 8], [0, 16]], 0, 1)
    SEL(M("IDN"), V("ONE", 0, 128), [[-1, 128]], 0, 1)
    IOTA(JW, [[16, 32]], 0, 0)
    IOTA(V("KC", 0, 4), [[16, 4]], 0, 0)
    IOTA(V("DM", 0, 64), [[0, 4], [1, 16]], 0, 0)
    IOTA(V("KR0", 0, 64), [[1, 64]], 0, 0)
    IOTA(V("K1R", 0, 64), [[1, 64]], 1, 0)
    IOTA(M("KT"), [[16, 4], [0, 32]], 0, 0)
    IOTA(V("MT", 0, 256), [[1, 8], [0, 32]], 0, 0)
    TS(PI(1), PI(0), 4, A_.arith_shift_right)
    TS(PI(2), PI(0), 15, A_.bitwise_and)
    TS(PI(3), PI(0), 1, A_.bitwise_and)
    TS(M("XE"), M("PAR"), 200.0, A_.mult)
    TS(M("XO"), M("PAR"), -200.0, A_.mult, 200.0, A_.add)
    CP(V("PF", 0, 4), V("PI", 0, 4))
    TT(M("XE"), M("XE"), M("X96"), A_.add)
    TT(M("XO"), M("XO"), M("X96"), A_.add)
    TS(M("G1"), M("CMG"), PF(1), A_.is_equal)

    def spread_rows(l):
        for r in (2 * l, 2 * l + 1, 6 + 2 * l, 7 + 2 * l):
            TS(V("SR1", 128 * r, 128 * r + 128), M("XE"), float(r), A_.is_equal)
            TS(V("SR2", 128 * r, 128 * r + 128), M("XO"), float(r), A_.is_equal)

    p96 = (0, 96)

    def spread_kids(l):
        for side in range(2):
            bank = "B%d" % (2 * (l % 2) + side)
            for half in range(2):
                r = 6 * side + 2 * l + half
                MM(V(bank, 256 * half, 256 * half + 256),
                   [(V("SR1", 128 * r, 128 * r + 128, 1, p96), V("F1", 0, 256, 1, p96)),
                    (V("SR2", 128 * r, 128 * r + 128, 1, p96), V("F2", 0, 256, 1, p96))])
            c = 1024 * l + 512 * side
            ACT(V("K", c, c + 512), V(bank, 0, 512))

    def types(l):
        MM(V("B7", 0, 512), [(V("Q3", 128 * l, 128 * l + 128, 1, (0, 24)), V("MRB", 0, 512, 1, (0, 24)))])

    spread_rows(0)
    TT(M("CMT"), M("G1"), M("CM1"), A_.mult)
    CP(V("F1", 0, 256, 1, p96), V("KR", 0, 256, 1, p96))
    TT(V("F2", 0, 256, 1, p96), V("KR", 0, 256, 1, p96), V("F1", 0, 256, 1, p96), A_.subtract)
    spread_kids(0)
    for l in range(3):
        TS(V("Q3", 128 * l, 128 * l + 128), M("XQ"), float(l), A_.is_equal)
    CP(V("MRB", 0, 512, 1, (0, 24)), V("MR", 0, 512, 1, (0, 24)))
    types(0)
    ACT(V("SGN", SOFF[0], SOFF[0] + 512), V("B7", *f), F_.Copy, -1.0, 2.0)
    for i in range(16):
        TS(L(i), M("CMT"), float(i + 1), A_.is_equal, 8.0, A_.mult)
    spread_rows(1)
    for nm, c in (("NI", -1.0), ("I128", 128.0), ("N256", -256.0), ("N254", -254.0), ("N2", -2.0), ("I255", 255.0)):
        TS(M(nm), M("IDN"), c, A_.mult)
    kid_lists(0, "B6")

    def more0():
        spread_kids(1)
        types(1)
        ACT(V("SGN", SOFF[1], SOFF[1] + 512), V("B7", *f), F_.Copy, -1.0, 2.0)
        kid_lists(1, "B6")
        spread_rows(2)

    TS(M("GP"), M("G1"), PF(2), A_.mult)
    level(0, more0)
    spread_kids(2)
    for i in range(16):
        SEL(V("LP", 128 * i, 128 * i + 128), M("GP"), [[0, 8], [1, 16]], -i, 0)

    def more1():
        types(2)
        ACT(V("SGN", SOFF[2], SOFF[2] + 512), V("B7", *f), F_.Copy, -1.0, 2.0)
        kid_lists(2, "B6")
        TT(V("MD0", *f), V("B7", *f), V("D0", *f), A_.mult)
        top_tables("B6")
        grandkids(0)

    level(1, more1)
    grandkids(1)
    diag(V("B7", 0, 64), "FFA", 0, 1024)
    TS(sub(GKF, 0, 64), V("B7", 0, 64), 1.0 / 64, A_.mult)

    def constants1():
        TS(M("NG"), M("G1"), -1.0, A_.mult)
        CP(M("G1F"), M("G1"))
        TS(M("GL"), M("CM1"), PF(2), A_.is_gt)
        TS(JW, JW, PF(2), A_.add)
        TS(V("KC", 0, 4), V("KC", 0, 4), PF(2), A_.add)
        TS(V("DM", 0, 64), V("DM", 0, 64), PF(2), A_.is_equal)
        TS(M("KT"), M("KT"), PF(2), A_.add)
        TS(PF(4), PF(2), 0.0, A_.is_equal)

    def constants2():
        TT(M("GL"), M("GL"), M("G1"), A_.mult)
        TS(V("CW", 0, 2), V("WTI", 0, 2), 0.125, A_.mult)
        FILL(V("YC", 512, 528), -1.0)
        FILL(V("PM", 0, 48), -1.0)
        FILL(V("KEYW", 0, 48), 0.0)
        FILL(V("DONW", 0, 48), 0.0)
        TS(V("KJ", 0, 4), V("KC", 0, 4), 3072.0, A_.add)
        TS(V("KC2", 0, 4), V("KC", 0, 4), 129.0 / 128, A_.mult, 3072.0, A_.add)
        TS(V("KR0", 0, 64), V("KR0", 0, 64), PF(4), A_.mult)
        TS(V("KOL", 0, 8), V("G1", 0, 128, 16), 0.125, A_.mult)

    CC = w(4)
    EA1, TB1, EM1, T5, DL, M1, COL, C1, LIVE, LV5, P5 = w(), w(), w(), w(), w(), w(), w(), w(), w(), w(), w()
    K2F, K2X, EA2, TB2, EM2, X1, X2, X3, DL2, E8, KY1, KY2 = w(64), w(64), w(), w(), w(), w(), w(), w(), w(), w(), w(), w()
    US, S1, S2, S4, CD8, RUN, BEST = w(), w(), w(64), w(128), w(256), w(64), w()
    SW, BI2, A1, A2, O1, O3, VA = w(4), w(4), w(4), w(4), w(4), w(4), w(4)
    I0, I1, I2, I3, I4, I5 = [V("WI", 32 * k, 32 * k + 32) for k in range(6)]
    SG0 = V("SGN", SOFF[2], SOFF[2] + 512)
    LW = V("LIBW", 0, 3840)

    for t in range(3):
        ACT(V("GA", *f), IND(V("Y", 0, 3328), V("KWU", 128, 160)))
        TT(V("NB", *f), IND(V("Y", 0, 3328), V("KWU", 160, 192)), SG0, A_.mult)

        def tail():
            if t == 0:
                grandkids(2)
            grandkids(3)
            TT(KD, sub(KAB, 32, 64), sub(KAB, 0, 32), A_.subtract)
            TT(CD, sub(CAB, 32, 64), sub(CAB, 0, 32), A_.subtract)
            if t == 0:
                constants2()
            else:
                a = 64 * (t - 1)
                CP(V("LIBW", a, a + 64), V("Y", a, a + 64))
                CP(V("LIBW", LIB + a, LIB + a + 64), V("Y", a, a + 64))

        kid_errors(V("D0", *f), V("MD0", *f), SG0, "WIN", 0, EA1, SCHED1, constants1 if t == 0 else None, tail)
        diag(V("B7", 64, 128), "FFB", 0, 1024)
        TT(TB1, V("B6", 0, 32), EA1, A_.is_lt)
        TT(M1, TB1, CD, A_.mult)
        TS(T5, TB1, 512.0, A_.mult)
        TT(COL, M1, sub(CAB, 0, 32), A_.add)
        TT(DL, T5, JW, A_.add)
        CP(V("LU", 0, 32), COL)
        ACT(V("SG2", *f), IND(V("SGN", 0, 1536), V("LU", 0, 32)))
        CP(V("DLU", 0, 32), DL)
        TS(sub(GKF, 64, 128), V("B7", 64, 128), 1.0 / 64, A_.mult)
        TT(GKD, sub(GKF, 64, 128), sub(GKF, 0, 64), A_.subtract)
        TT(sub(K2X, 0, 32), TB1, sub(GKD, 0, 32), A_.mult)
        TT(sub(K2X, 32, 64), TB1, sub(GKD, 32, 64), A_.mult)
        TT(EM1, V("B6", 0, 32), EA1, A_.min)
        TT(K2F, K2X, sub(GKF, 0, 64), A_.add)
        TT(M1, TB1, KD, A_.mult)
        CP(V("K2U", 0, 64), K2F)
        CP(V("WIN2", *f), IND(V("WIN", 0, 1024), V("DLU", 0, 32)))
        ACT(V("GA", *f), IND(V("Y", 0, 2816), V("K2U", 0, 32)))
        TT(V("NB", *f), IND(V("Y", 0, 2816), V("K2U", 32, 64)), V("SG2", *f), A_.mult)
        TT(C1, M1, sub(KAB, 0, 32), A_.add)

        def tail2():
            TS(LIVE, C1, float(NODE0), A_.is_ge)
            TT(X3, sub(K2F, 32, 64), sub(K2F, 0, 32), A_.subtract)
            TS(LV5, LIVE, 512.0, A_.mult)
            TS(KY1, DL, 2048.0, A_.add)
            TT(P5, LV5, JW, A_.add)

        kid_errors(V("WIN2", *f), V("MD", *f), V("SG2", *f), "WIN2", 512, EA2, SCHED2, None, tail2)
        TT(TB2, V("B6", 0, 32), EA2, A_.is_lt)
        TT(EM2, V("B6", 0, 32), EA2, A_.min)
        TT(X1, TB2, LV5, A_.mult)
        TT(X3, X3, TB2, A_.mult)
        TT(DL2, X1, P5, A_.add)
        TT(EM2, EM2, EM1, A_.subtract)
        CP(V("LU", 32, 64), DL2)
        W2 = IND(V("WIN2", 0, 1536), V("LU", 32, 64))
        ACT(V("DC", 0, 512), W2, F_.Copy, None, V("CW", 0, 1))
        TS(V("DC", 512, 1024), W2, V("CW", 1, 2), A_.mult)
        ACT(V("DN", *f), W2)
        diag(V("B7", 0, 64), "DC", 0, 1024)
        TT(X3, X3, sub(K2F, 0, 32), A_.add)
        TT(EM2, EM2, LIVE, A_.mult)
        TT(X3, X3, C1, A_.subtract)
        TT(E8, EM2, EM1, A_.add)
        TT(X3, X3, LIVE, A_.mult)
        TS(KY2, TB2, 512.0, A_.mult)
        TT(X3, X3, C1, A_.add)
        TS(US, V("B7", 0, 32), 32.0, A_.add)
        TS(I3, V("B7", 0, 32), 0.0, A_.add)
        TT(I0, V("B7", 32, 64), US, A_.mult)
        TS(I4, I3, 127, A_.bitwise_and)
        TS(I5, I0, 5, A_.arith_shift_right, 2047, A_.bitwise_and)
        TS(S1, I4, 2.0, A_.mult, 1.0, A_.add)
        CP(V("CU", 0, 32), I5)
        ACT(V("CG", 0, 512), IND(LW, V("CU", 0, 32)))
        CP(sub(CD8, 0, 32), I5)
        TS(sub(S2, 0, 32), I4, 4.0, A_.mult, 2.0, A_.add)
        TS(sub(S2, 32, 64), I4, 4.0, A_.mult, 2.0, A_.add)
        TT(sub(CD8, 32, 64), sub(CD8, 0, 32), S1, A_.add)
        CP(V("CHU", 0, 32), X3)
        TT(sub(CD8, 64, 128), sub(CD8, 0, 64), S2, A_.add)
        CP(V("CU", 32, 64), sub(CD8, 32, 64))
        CP(V("CU", 64, 128), sub(CD8, 64, 128))
        ACT(V("CG", 512, 1024), IND(LW, V("CU", 32, 64)))

        def cand(m, buf):
            TT(V(buf, 512 * (m % 2), 512 * (m % 2) + 512), IND(LW, V("CU", 32 * m, 32 * m + 32)), V("DN", *f), A_.subtract)

        cand(2, "XA0")
        for h in range(2):
            MM(V("B%d" % (2 + h), *f), [(M("NI"), V("DN", *f)), (M("IDN"), V("CG", 512 * h, 512 * h + 512))])
            ACT(V("AC0", 512 * h, 512 * h + 512), V("B%d" % (2 + h), *f), F_.Abs)
        diag(V("B5", 0, 64), "AC0", 0, 1024, [(M("IDN"), V("MT", 0, 64))])
        TS(sub(S4, 0, 64), S2, 2.0, A_.mult)
        TS(sub(S4, 64, 128), S2, 2.0, A_.mult)
        cand(3, "XA0")
        ACT(V("AC1", 0, 1024), V("XA0", 0, 1024), F_.Abs)
        diag(V("B6", 0, 64), "AC1", 0, 1024, [(M("IDN"), V("MT", 64, 128))])
        TT(sub(CD8, 128, 256), sub(CD8, 0, 128), S4, A_.add)
        CP(V("CU", 128, 256), sub(CD8, 128, 256))
        cand(4, "XA1")
        CP(RUN, V("B5", 0, 64))
        cand(5, "XA1")
        ACT(V("AC2", 0, 1024), V("XA1", 0, 1024), F_.Abs)
        diag(V("B5", 0, 64), "AC2", 0, 1024, [(M("IDN"), V("MT", 128, 192))])
        cand(6, "XA2")
        ACT(V("AC3", 0, 512), V("XA2", 0, 512), F_.Abs)
        diag(V("B7", 0, 32), "AC3", 0, 512, [(M("IDN"), V("MT", 192, 224))])
        TT(RUN, V("B6", 0, 64), RUN, A_.min)
        cand(7, "XA2")
        ACT(V("AC3", 512, 1024), V("XA2", 512, 1024), F_.Abs)
        diag(V("B6", 0, 32), "AC3", 512, 1024, [(M("IDN"), V("MT", 224, 256))])
        ACT(V("YC", *f), IND(V("Y", 0, 3840), V("CHU", 0, 32)) if t > 5 else IND(V("Y", 0, 3328), V("CHU", 0, 32)))
        TT(RUN, V("B5", 0, 64), RUN, A_.min)
        TT(KY2, KY2, COL, A_.add)
        TT(sub(RUN, 0, 32), sub(RUN, 0, 32), sub(RUN, 32, 64), A_.min)
        TT(KY2, KY2, KY1, A_.subtract)
        TT(sub(RUN, 0, 32), V("B7", 0, 32), sub(RUN, 0, 32), A_.min)
        TT(KY2, KY2, LIVE, A_.mult)
        TT(KY2, KY2, KY1, A_.add)
        TS(V("KEYW", 0, 32), KY2, 128.0, A_.mult)
        TT(BEST, V("B6", 0, 32), sub(RUN, 0, 32), A_.min)
        TT(V("BB", 0, 32), BEST, E8, A_.is_lt)
        CP(I0, BEST)
        op("v", [("ONE", 0, 32), ("BB", 0, 32)], [("INC", 0, 32)],
           lambda: g.vector.tensor_tensor_scan(T.INC[:, 0:32], T.ONE[:, 0:32], T.BB[:, 0:32], 0.0, A_.mult, A_.add))
        TS(I1, I0, 7, A_.bitwise_and)
        for q in range(4):
            MM(V("B0", 32 * q, 32 * q + 32), [(M("G1"), V("INC", 0, 32))])
        MM(V("B1", 0, 32), [(M("NG"), V("BB", 0, 32)), (M("GL"), V("BB", 0, 32)), (M("G1"), V("INC", 0, 32))])
        TT(X1, I1, S1, A_.mult)
        TT(M("CMP"), V("B0", 0, 128), M("KT"), A_.is_le)
        TT(V("PM", 0, 32), V("B1", 0, 32), V("BB", 0, 32), A_.mult)
        for q in range(4):
            RED(sub(CC, q, q + 1), V("CMP", 32 * q, 32 * q + 32))
        TT(X1, X1, sub(CD8, 0, 32), A_.add)
        CP(V("CCU", 0, 4), CC)
        TS(V("CC16", 0, 4), CC, 16.0, A_.mult)
        TT(V("OH", 0, 64), IND(V("PM", 0, 48), V("CCU", 0, 4)), V("K1R", 0, 64), A_.is_equal)
        MM(V("B2", 0, 4), [(M("IDN"), V("CC16", 0, 4))] + [(V("LP", 128 * i, 128 * i + 128), V("OH", i, 64, 16)) for i in range(16)])
        TS(X2, X1, 2048.0, A_.is_ge, 2048.0, A_.mult)
        TT(V("DONW", 0, 32), X1, X2, A_.subtract)
        TT(V("VK", 0, 64), IND(V("KEYW", 0, 48), V("CCU", 0, 4)), V("OH", 0, 64), A_.mult)
        TS(VA, CC, 32.0, A_.is_lt)
        CP(V("JLU", 0, 4), V("B2", 0, 4))
        SND = "SND%d" % t
        CP(V(SND, 0, 64), IND(V("YC", 0, 528), V("JLU", 0, 4)))
        waits("g", [(SND, 0, 64)], [])
        land = "LAND%d" % t if hop is None else "RLY%d" % t
        g.remote_dma(T[land][:], T[SND][:], T.sem[("arr%d" if hop is None else "hop%d") % t], T.sem["snt%d" % t], spid, srid, smask)
        TT(V("VD", 0, 64), IND(V("DONW", 0, 48), V("CCU", 0, 4)), V("OH", 0, 64), A_.mult)
        MM(V("B3", 0, 64), [(M("G1F"), V("KR0", 0, 64)), (M("G1F"), V("VK", 0, 64))])
        MM(V("B7", 0, 64), [(M("G1F"), V("VD", 0, 64))])
        TT(V("SWT", 0, 64), V("B3", 0, 64), V("DM", 0, 64), A_.mult)
        CP(V("ROWS", 0, 64), V("B3", 0, 64))
        for q in range(4):
            RED(sub(SW, q, q + 1), V("SWT", 16 * q, 16 * q + 16))
        TS(BI2, SW, -63.5, A_.add)
        for q in range(4):
            TS(V("CMQ", 64 * q, 64 * q + 64), V("ROWS", 0, 64), sub(SW, q, q + 1), A_.is_lt)
            ACT(V("SGJ", 0, 64), V("ROWS", 0, 64), F_.Sign, sub(BI2, q, q + 1), -1.0, sub(A2, q, q + 1))
        for q in range(4):
            RED(sub(A1, q, q + 1), V("CMQ", 64 * q, 64 * q + 64))
        TS(O1, SW, 1.0 / 128, A_.mult)
        TS(V("TQ", 0, 64), V("B7", 0, 64), PF(3), A_.mult)
        TS(O3, A1, 2.0, A_.mult, -64.0, A_.add)
        TT(O1, O1, V("KC2", 0, 4), A_.subtract)
        TT(V("SRC", 0, 64), V("B7", 0, 64), V("TQ", 0, 64), A_.subtract)
        TT(O1, O1, VA, A_.mult)
        TT(O3, A2, O3, A_.is_equal)
        TT(O1, O1, O3, A_.mult)
        TT(O1, O1, V("KJ", 0, 4), A_.add)
        CP(V("OFU", 0, 4), O1)
        op("v", [("SRC", 0, 64), ("OFU", 0, 4)], [("K", 0, 3136)],
           lambda: g.vector.tensor_copy(out=T.K[:, 0:3136].indirect(T.OFU[:, 0:4]), in_=T.SRC[:, 0:64]))
        kid_lists(0, "B4")
        kid_lists(2, "B6")
        if t < 2:
            top_tables("B6")
            grandkids(0)
        kid_lists(1, "B5")
        a = 64 * t
        g.vector.wait_ge(T.sem["arr%d" % t], acnt)
        lnd = V("LAND%d" % t, 0, 64)
        TS(V("MGM", 0, 64), lnd, 0.0, A_.is_lt)
        TT(V("MGO", 0, 64), V("Y", a, a + 64), V("MGM", 0, 64), A_.mult)
        TT(V("Y", a, a + 64), lnd, V("MGO", 0, 64), A_.max)
        if t < 2:
            level(0, lambda: grandkids(1))
            diag(V("B7", 0, 64), "FFA", 0, 1024)
            level(1, lambda: grandkids(2))
            TS(sub(GKF, 0, 64), V("B7", 0, 64), 1.0 / 64, A_.mult)
        else:
            def kids_out(l):
                for side in range(2):
                    c, o, bank, p8 = 1024 * l + 512 * side, 1536 * side + 512 * l, "B%d" % (5 + side), (0, 8)
                    MM(V(bank, 0, 512, 1, p8), [(V("KOL", 0, 8), V("K", c, c + 512))])
                    ACT(V("KOB", o, o + 512, 1, p8), V(bank, 0, 512, 1, p8))
            DMA("s", T.yo[:, 0:NODE0], T.Y[:, 0:NODE0], [("Y", 0, NODE0)], [])
            for l in range(3):
                level(l, lambda: kids_out(l))
                if l == 2:
                    DMA("s", T.ko[:], T.KOB[0:8, :], [("KOB", 0, 3072)], [])
                h = NODE0 + 512 * l
                DMA("s", T.yo[:, h:h + 512], T.Y[:, h:h + 512], [("Y", h, h + 512)], [])

    for t in range(3):
        g.wait_ge(T.sem["snt%d" % t], scnt)
    for k in range(nd[0]):
        g.sync.wait_ge(T.sem["d%d" % k], 16)
    for q in ("v", "a", "p", "g"):
        g.sync.wait_ge(T.sem["q" + q], cnt[q])
